import numpy as np
import ml_dtypes


def mxq(x, axis, fmt="e4m3"):
    dtype, down = {"e4m3": (ml_dtypes.float8_e4m3fn, 7), "e5m2": (ml_dtypes.float8_e5m2, 14)}[fmt]
    v = np.moveaxis(np.asarray(x, np.float32).astype(ml_dtypes.bfloat16).astype(np.float64), axis, -1)
    blocks = v.reshape(v.shape[:-1] + (-1, 32))
    amax = np.abs(blocks).max(-1, keepdims=True)
    byte = np.maximum(np.where(amax > 0, np.frexp(amax)[1] - 1 + 127, 0) - down, 1)
    scale = np.exp2(byte - 127.0)
    codes = (blocks / scale).astype(np.float32).astype(dtype).astype(np.float64)
    return np.moveaxis((codes * scale).reshape(v.shape), -1, axis)


WIDE = False


def mx_kscale(k):
    if not WIDE:
        return np.ones(k)
    levels = np.array([30, -30])
    if k % 512:
        return np.exp2(np.random.permutation(np.resize(levels, k // 32))).repeat(32)
    a = np.empty((k // 512, 16))
    for p in range(k // 512):
        a[p, :8] = np.random.permutation(np.resize(levels, 8))
        for g in range(8):
            far = levels[np.abs(levels - a[p, g]) >= 10]
            a[p, g + 8] = far[np.random.randint(len(far))]
    return np.exp2(a.ravel()).repeat(32)


BF16 = ml_dtypes.bfloat16


def bf(x):
    return np.asarray(x, np.float32).astype(BF16)


def f64(x):
    return np.asarray(x).astype(np.float64)


B, S, C, E = 4, 256, 512, 3072


def hard_swish(v):
    return v * np.minimum(np.maximum(v + 3.0, 0.0), 6.0) / 6.0


def sigmoid(v):
    return 1.0 / (1.0 + np.exp(-v))


def setup_inputs():
    s, t = mx_kscale(C), mx_kscale(E)
    contrast = np.random.uniform(0.6, 1.4, (B, 1, 1))
    x = np.random.standard_normal((B, S, C)) * contrast
    return {"x": bf(x.reshape(B * S, C)),
            "in_gain": bf((1 + 0.1 * np.random.standard_normal(C)) * s),
            "in_bias": bf(0.3 * np.random.standard_normal(C) * s),
            "we": bf(2 * np.random.standard_normal((C, E)) / np.sqrt(C) / s[:, None]),
            "be": bf(0.5 * np.random.standard_normal(E)),
            "alpha": bf(1 + 0.3 * np.random.standard_normal(E)),
            "beta": bf(0.5 * np.random.standard_normal(E) - 1),
            "lam": bf((1 + 0.1 * np.random.standard_normal(E)) * t),
            "wp": bf(np.random.standard_normal((E, C)) / np.sqrt(E) / t[:, None]),
            "bp": bf(0.3 * np.random.standard_normal(C))}


def reference(x, in_gain, in_bias, we, be, alpha, beta, lam, wp, bp):
    xf = f64(x)
    u = xf * f64(in_gain) + f64(in_bias)
    e = mxq(u, 1, "e4m3") @ mxq(f64(we), 0, "e4m3")
    a = hard_swish(e + f64(be)).reshape(B, S, E)
    energy = np.sqrt(np.mean(a * a, axis=1))
    gate = sigmoid(f64(alpha) * energy + f64(beta)) * f64(lam)
    h = (a * gate[:, None, :]).reshape(B * S, E)
    y = mxq(h, 1, "e5m2") @ mxq(f64(wp), 0, "e4m3")
    return xf + y + f64(bp)

@@ -1,0 +1,406 @@
+from contextlib import ExitStack
+
+import concourse.mybir as mybir
+from concourse.masks import make_identity
+
+B, S, C, E = 4, 256, 512, 3072
+FLOPS = 2 * 2 * B * S * C * E
+
+F32 = mybir.dt.float32
+BF16 = mybir.dt.bfloat16
+U32 = mybir.dt.uint32
+U8 = mybir.dt.uint8
+E4X4 = mybir.dt.float8_e4m3fn_x4
+E5X4 = mybir.dt.float8_e5m2_x4
+ALU = mybir.AluOpType
+ACT = mybir.ActivationFunctionType
+
+P = 128
+G = 6
+HALF = 512
+UNITS = 2 * G
+TILES = 4 * UNITS
+LAST = UNITS - 1
+
+ROW_GAIN, ROW_BIAS, ROW_BE, ROWS_FIRST = 0, 1, 2, 8
+ROW_ALPHA, ROW_BETA, ROW_LAM, ROW_BP, ROWS_LATER = 0, 6, 12, 18, 18
+
+
+def tile_gated_inverted_bottleneck_f3_kernel(
+    tc, x, in_gain, in_bias, we, be, alpha, beta, lam, wp, bp, out
+):
+    nc = tc.nc
+    with ExitStack() as ctx:
+        keep = ctx.enter_context(tc.tile_pool(name="keep", bufs=1))
+        work = ctx.enter_context(tc.tile_pool(name="work", bufs=2))
+        bankp = ctx.enter_context(tc.psum_pool(name="bankp", bufs=4))
+        accp = ctx.enter_context(tc.psum_pool(name="accp", bufs=4))
+        ctx.enter_context(tc.manual_schedule())
+
+        rows_first = keep.tile([P, C], BF16, name="rows_first")
+        rows_later = keep.tile([P, C], BF16, name="rows_later")
+        nc.vector.memset(rows_first[:], 0.0)
+        nc.vector.memset(rows_later[:], 0.0)
+        ident_f = keep.tile([P, P], F32, name="ident_f")
+        ident_b = keep.tile([P, P], BF16, name="ident_b")
+        half_exp = keep.tile([P, 8], F32, name="half_exp")
+        nc.gpsimd.memset(half_exp[:], 0.5)
+        one = keep.tile([P, 1], F32, name="one")
+        nc.gpsimd.memset(one[:], 1.0)
+        make_identity(nc, ident_f[:])
+        make_identity(nc, ident_b[:])
+
+        def load_row(queue, tile, vec, row, g0, g1):
+            queue.dma_start(out=tile[row + g0 : row + g1, :], in_=vec.rearrange("(g c) -> g c", c=C)[g0:g1])
+
+        for vec, row in ((alpha, ROW_ALPHA), (beta, ROW_BETA), (lam, ROW_LAM)):
+            load_row(nc.gpsimd, rows_later, vec, row, 0, G)
+        load_row(nc.gpsimd, rows_later, bp, ROW_BP, 0, 1)
+        warm = keep.tile([P, 1], F32, name="warm")
+        nc.scalar.activation(out=warm[:], in_=one[:], func=ACT.Sigmoid)
+        x_sb = []
+        we_raw = []
+        wp_raw = []
+        x_view = x.rearrange("(b p i) c -> b p i c", p=P, i=2)
+        we_view = we.rearrange("(p j) e -> p j e", j=4)
+        wp_view = wp.rearrange("(g p j) c -> g p j c", p=P, j=4)
+
+        def load_x(b):
+            t = keep.tile([P, 2, C], BF16, name="x%d" % b)
+            nc.sync.dma_start(out=t[:], in_=x_view[b])
+            x_sb.append(t)
+
+        def load_we(g):
+            t = keep.tile([P, 4, 512], BF16, name="we_raw%d" % g)
+            nc.sync.dma_start(out=t[:], in_=we_view[:, :, 512 * g : 512 * g + 512])
+            we_raw.append(t)
+
+        def load_wp(g):
+            t = keep.tile([P, 4, C], BF16, name="wp_raw%d" % g)
+            nc.sync.dma_start(out=t[:], in_=wp_view[g])
+            wp_raw.append(t)
+
+        load_row(nc.sync, rows_first, in_gain, ROW_GAIN, 0, 1)
+        load_row(nc.sync, rows_first, in_bias, ROW_BIAS, 0, 1)
+        load_x(0)
+        load_x(1)
+        load_row(nc.sync, rows_first, be, ROW_BE, 0, 4)
+        load_row(nc.sync, rows_first, be, ROW_BE, 4, G)
+        load_we(0)
+        load_x(2)
+        load_x(3)
+        load_we(1)
+        load_wp(0)
+        for g in range(2, G):
+            load_we(g)
+            load_wp(g - 1)
+        load_wp(G - 1)
+
+        def transposed_rows(rows, count, label):
+            words = rows[:].bitcast(F32)
+            pt = accp.tile([P, 2 * P], F32, name="pt", tag="acc")
+            for u in range(2):
+                nc.tensor.transpose(pt[:, P * u : P * u + P], words[:, u::2], ident_f[:])
+            par = keep.tile([P, count, 4], F32, name=label)
+            nc.vector.tensor_copy(
+                out=par[:].rearrange("p r (u e) -> p r u e", e=2),
+                in_=pt[:].bitcast(BF16).rearrange("p (u r e) -> p r u e", u=2, e=2)[:, :count],
+            )
+            return par
+
+        be_up = keep.tile([P, G, 4], F32, name="be_up")
+        be_dn = keep.tile([P, G, 4], F32, name="be_dn")
+
+        u_codes = keep.tile([P, B * S], U32, name="u_codes", align_bytes=64)
+        u_scales = keep.tile([P, B * S], U8, name="u_scales", align_bytes=64)
+        we_codes = keep.tile([P, E], U32, name="we_codes", align_bytes=64)
+        we_scales = keep.tile([P, E], U8, name="we_scales", align_bytes=64)
+        wp_codes = keep.tile([P, G, C], U32, name="wp_codes", align_bytes=64)
+        wp_scales = keep.tile([P, G, C], U8, name="wp_scales", align_bytes=64)
+        xb = keep.tile([P, 2 * B, C], F32, name="xb")
+        bp_all = keep.tile([P, C], F32, name="bp_all")
+
+        xt = {}
+        ut = {}
+
+        def x_transposes(n):
+            for u in range(2):
+                t = accp.tile([P, HALF], F32, name="xt", tag="acc")
+                for j in range(4):
+                    words = x_sb[2 * n + j // 2][:].rearrange("p i c -> p (i c)").bitcast(F32)
+                    w0 = (C // 2) * (j % 2)
+                    nc.tensor.transpose(t[:, P * j : P * j + P], words[:, w0 + u : w0 + C // 2 : 2], ident_f[:])
+                xt[n, u] = t
+
+        def affine(n, t):
+            if n not in ut:
+                u_tile = work.tile([P, 4, HALF], BF16, name="ut", tag="ut")
+                ut[n] = u_tile
+            u, e = divmod(t, 2)
+            src = xt[n, u][:].bitcast(BF16).rearrange("p (c e) -> p e c", e=2)[:, e, :]
+            dst = ut[n][:, t, :]
+            gain = par_first[:, ROW_GAIN, t : t + 1]
+            bias = par_first[:, ROW_BIAS, t : t + 1]
+            if u == 1:
+                nc.scalar.activation(out=dst, in_=src, func=ACT.Identity, scale=gain, bias=bias)
+            else:
+                nc.vector.tensor_scalar(out=dst, in0=src, scalar1=gain, scalar2=bias, op0=ALU.mult, op1=ALU.add)
+
+        ui = {}
+
+        def u_interleave(n):
+            t = work.tile([P, 4 * HALF], BF16, name="ui", tag="ui", align_bytes=64)
+            nc.vector.tensor_copy(
+                out=t[:].rearrange("p (c i t) -> p c t i", i=4, t=4),
+                in_=ut[n][:].rearrange("p t (c i) -> p c t i", i=4),
+            )
+            ui[n] = t
+
+        def u_quantize(n):
+            cols = slice(HALF * n, HALF * n + HALF)
+            nc.vector.quantize_mx(out=u_codes[:, cols].bitcast(E4X4), scales=u_scales[:, cols], in_=ui[n][:])
+
+        wi = {}
+
+        def wi_tile(kind, g):
+            if (kind, g) not in wi:
+                t = work.tile([P, 2048], BF16, name="wi_" + kind, tag="wi_" + kind, align_bytes=64)
+                wi[kind, g] = t
+            return wi[kind, g]
+
+        def weight_pe(kind, g, h):
+            bank = bankp.tile([P, 1024], BF16, name="bank", tag="bank")
+            for q in (2 * h, 2 * h + 1):
+                if kind == "we":
+                    view = we_raw[g][:].rearrange("p j (m t) -> p t m j", t=4)[:, q]
+                else:
+                    view = wp_raw[g][:, :, P * q : P * q + P].rearrange("p j c -> p c j")
+                o = 512 * (q % 2)
+                nc.tensor.matmul(bank[:, o : o + 512], lhsT=ident_b[:], rhs=view, start=True, stop=True)
+            nc.scalar.copy(out=wi_tile(kind, g)[:, 1024 * h : 1024 * h + 1024], in_=bank[:])
+
+        def wp_vector(g):
+            nc.vector.tensor_copy(
+                out=wi_tile("wp", g)[:, 1024:].rearrange("p (c i j) -> p c j i", i=4, j=4),
+                in_=wp_raw[g][:, :, 256:].rearrange("p j (c i) -> p c j i", i=4),
+            )
+
+        def we_quantize(g):
+            cols = slice(512 * g, 512 * g + 512)
+            nc.vector.quantize_mx(out=we_codes[:, cols].bitcast(E4X4), scales=we_scales[:, cols], in_=wi["we", g][:])
+
+        def wp_quantize(g):
+            nc.vector.quantize_mx(out=wp_codes[:, g, :].bitcast(E4X4), scales=wp_scales[:, g, :], in_=wi["wp", g][:])
+
+        e_ps = {}
+        r_sb = {}
+        c_sb = {}
+        a_sb = {}
+        ms_sb = {}
+        z_sb = {}
+        gate_sb = {}
+        h_sb = {}
+        hq = {}
+        acc = {}
+
+        def expand(T):
+            i, t = divmod(T, 4)
+            n, g = divmod(i, G)
+            bank = bankp.tile([P, HALF], F32, name="bank_e", tag="bank")
+            m = slice(512 * g + P * t, 512 * g + P * t + P)
+            k = slice(HALF * n, HALF * n + HALF)
+            nc.tensor.matmul_mx(
+                out=bank[:], lhsT=we_codes[:, m].bitcast(E4X4), lhsT_scale=we_scales[:, m],
+                rhs=u_codes[:, k].bitcast(E4X4), rhs_scale=u_scales[:, k], start=True, stop=True,
+            )
+            e_ps[T] = bank
+
+        def on_scalar(T):
+            return T % 4 == 2
+
+        def ramp(T):
+            i, t = divmod(T, 4)
+            g = i % G
+            r = work.tile([P, HALF], F32, name="r", tag="r", bufs=4)
+            if on_scalar(T):
+                nc.scalar.activation(out=r[:], in_=e_ps[T][:], func=ACT.Relu, scale=-1.0 / 6.0, bias=be_dn[:, g, t : t + 1])
+            else:
+                nc.scalar.activation(out=r[:], in_=e_ps[T][:], func=ACT.Relu, scale=1.0 / 6.0, bias=be_up[:, g, t : t + 1])
+            r_sb[T] = r
+
+        def clip(T):
+            c = work.tile([P, HALF], F32, name="c", tag="c", bufs=4)
+            if on_scalar(T):
+                nc.scalar.activation(out=c[:], in_=r_sb[T][:], func=ACT.Relu, scale=-1.0, bias=one[:])
+            else:
+                nc.vector.tensor_scalar(out=c[:], in0=r_sb[T][:], scalar1=1.0, scalar2=None, op0=ALU.min)
+            c_sb[T] = c
+
+        def swish(T):
+            i, t = divmod(T, 4)
+            if t == 0:
+                a = work.tile([P, 4, HALF], F32, name="a", tag="a", bufs=3)
+                a_sb[i] = a
+            nc.vector.scalar_tensor_tensor(
+                out=a_sb[i][:, t, :], in0=e_ps[T][:], scalar=par_first[:, ROW_BE + i % G, t : t + 1], in1=c_sb[T][:],
+                op0=ALU.add, op1=ALU.mult,
+            )
+
+        def square(T):
+            i, t = divmod(T, 4)
+            if t == 0:
+                ms = work.tile([P, 2, 4], F32, name="ms", tag="ms")
+                ms_sb[i] = ms
+            for b in range(2):
+                junk = work.tile([P, S], F32, name="junk", tag="junk")
+                nc.scalar.activation(
+                    out=junk[:], in_=a_sb[i][:, t, S * b : S * b + S], func=ACT.Square, scale=1.0 / 16.0,
+                    accum_out=ms_sb[i][:, b, t : t + 1],
+                )
+
+        def over_images(row, i):
+            return par_later[:, row + i % G, :].unsqueeze(1).to_broadcast([P, 2, 4])
+
+        def gate_in(i):
+            z = work.tile([P, 2, 4], F32, name="z", tag="z")
+            z1 = work.tile([P, 2, 4], F32, name="z1", tag="z1")
+            z2 = work.tile([P, 2, 4], F32, name="z2", tag="z2")
+            nc.gpsimd.tensor_tensor(out=z[:], in0=ms_sb[i][:], in1=half_exp[:].rearrange("p (b t) -> p b t", t=4), op=ALU.pow)
+            nc.gpsimd.tensor_tensor(out=z1[:], in0=z[:], in1=over_images(ROW_ALPHA, i), op=ALU.mult)
+            nc.gpsimd.tensor_tensor(out=z2[:], in0=z1[:], in1=over_images(ROW_BETA, i), op=ALU.add)
+            z_sb[i] = z2
+
+        def gate_out(i):
+            sg = work.tile([P, 2, 4], F32, name="sg", tag="sg")
+            gate = work.tile([P, 2, 4], F32, name="gate", tag="gate")
+            nc.scalar.activation(out=sg[:], in_=z_sb[i][:], func=ACT.Sigmoid)
+            nc.gpsimd.tensor_tensor(out=gate[:], in0=sg[:], in1=over_images(ROW_LAM, i), op=ALU.mult)
+            gate_sb[i] = gate
+
+        def gated(i, b):
+            if b == 0:
+                h = work.tile([P, 2, S, 4], BF16, name="h", tag="h", align_bytes=64)
+                h_sb[i] = h
+            nc.vector.tensor_tensor(
+                out=h_sb[i][:, b],
+                in0=a_sb[i][:, :, S * b : S * b + S].rearrange("p t n -> p n t"),
+                in1=gate_sb[i][:, b, :].unsqueeze(1).to_broadcast([P, S, 4]),
+                op=ALU.mult,
+            )
+
+        def h_quantize(i, b0, b1):
+            if b0 == 0:
+                codes = work.tile([P, HALF], U32, name="h_codes", tag="h_codes", align_bytes=64)
+                scales = work.tile([P, HALF], U8, name="h_scales", tag="h_scales", align_bytes=64)
+                hq[i] = (codes, scales)
+            codes, scales = hq[i]
+            cols = slice(S * b0, S * b1)
+            nc.vector.quantize_mx(
+                out=codes[:, cols].bitcast(E5X4), scales=scales[:, cols],
+                in_=h_sb[i][:].rearrange("p b n t -> p (b n t)")[:, 4 * S * b0 : 4 * S * b1],
+            )
+
+        def project(i):
+            n, g = divmod(i, G)
+            codes, scales = hq[i]
+            for j in range(4):
+                if g == 0:
+                    t = accp.tile([P, C], F32, name="acc", tag="acc")
+                    acc[n, j] = t
+                m = slice(P * j, P * j + P)
+                nc.tensor.matmul_mx(
+                    out=acc[n, j][:], lhsT=codes[:, m].bitcast(E5X4), lhsT_scale=scales[:, m],
+                    rhs=wp_codes[:, g, :].bitcast(E4X4), rhs_scale=wp_scales[:, g, :],
+                    start=(g == 0), stop=(g == G - 1),
+                )
+
+        out_view = out.rearrange("(b p i) c -> b i p c", p=P, i=2)
+
+        def finish(n, j):
+            o = work.tile([P, C], F32, name="o", tag="o", bufs=4)
+            nc.vector.tensor_tensor(out=o[:], in0=acc[n, j][:], in1=xb[:, 4 * n + j, :], op=ALU.add)
+            nc.sync.dma_start(out=out_view[2 * n + j // 2, j % 2], in_=o[:])
+
+        x_transposes(0)
+        par_first = transposed_rows(rows_first, ROWS_FIRST, "par_first")
+        affine(0, 2)
+        affine(0, 0)
+        affine(0, 3)
+        affine(0, 1)
+        weight_pe("we", 0, 0)
+        weight_pe("we", 0, 1)
+        be_par = par_first[:, ROW_BE : ROW_BE + G, :]
+        nc.vector.tensor_scalar(out=be_up[:], in0=be_par, scalar1=1.0 / 6.0, scalar2=0.5, op0=ALU.mult, op1=ALU.add)
+        nc.vector.tensor_scalar(out=be_dn[:], in0=be_par, scalar1=-1.0 / 6.0, scalar2=0.5, op0=ALU.mult, op1=ALU.add)
+        u_interleave(0)
+        we_quantize(0)
+        u_quantize(0)
+
+        for s in range(-2, TILES + 8):
+            i, t = divmod(s, 4)
+            if s + 2 < TILES:
+                expand(s + 2)
+            if t == 1 and 0 <= i - 2 < UNITS:
+                project(i - 2)
+            if s == 0:
+                x_transposes(1)
+            if s == 1:
+                par_later = transposed_rows(rows_later, ROWS_LATER, "par_later")
+                bp_ps = accp.tile([P, C], F32, name="bp_ps", tag="acc")
+                picked = ident_b[:, ROW_BP : ROW_BP + 1].to_broadcast([P, P])
+                nc.tensor.matmul(bp_ps[:], lhsT=picked, rhs=rows_later[:], start=True, stop=True)
+                nc.scalar.copy(out=bp_all[:], in_=bp_ps[:])
+            if 0 <= s - 1 < TILES:
+                square(s - 1)
+            if s + 2 < TILES:
+                ramp(s + 2)
+            if t == 0 and 0 <= i - 1 < UNITS:
+                gate_in(i - 1)
+            if t == 1 and 0 <= i - 1 < UNITS:
+                gate_out(i - 1)
+            if t == 2 and 0 <= i < 8:
+                nc.gpsimd.tensor_tensor(out=xb[:, i, :], in0=x_sb[i // 2][:, i % 2, :], in1=bp_all[:], op=ALU.add)
+            if 0 <= s < TILES:
+                swish(s)
+            if 0 <= s + 1 < TILES:
+                clip(s + 1)
+            if t == 0 and 0 <= i - 2 < LAST:
+                h_quantize(i - 2, 0, 2)
+            if t == 0 and i < G:
+                wp_vector(i)
+            if t == 1 and i == 0:
+                affine(1, 2)
+                affine(1, 0)
+                affine(1, 3)
+                affine(1, 1)
+            if t == 2 and i == 0:
+                u_interleave(1)
+            if t == 3 and i == 0:
+                u_quantize(1)
+            if t == 3 and 0 < i + 2 < G:
+                weight_pe("we", i + 2, 0)
+            if t == 0 and 0 < i + 1 < G:
+                weight_pe("we", i + 1, 1)
+            if t == 2 and 0 <= i < G:
+                weight_pe("wp", i, 0)
+            if t == 1 and 0 <= i - 1 < G:
+                wp_quantize(i - 1)
+            if t == 1 and 0 < i + 1 < G:
+                we_quantize(i + 1)
+            if t == 2 and 0 <= i - 1 < UNITS:
+                gated(i - 1, 0)
+            if t == 3 and 0 <= i - 1 < UNITS:
+                gated(i - 1, 1)
+                if i - 1 == LAST:
+                    h_quantize(LAST, 0, 1)
+            if t == 0 and i - 2 == LAST:
+                h_quantize(LAST, 1, 2)
+            if (i, t) == (7, 2):
+                finish(0, 0)
+            if (i, t) == (7, 3):
+                finish(0, 1)
+            if (i, t) == (8, 0):
+                finish(0, 2)
+                finish(0, 3)
+        for j in range(4):
+            finish(1, j)

@@ -108,8 +108,8 @@ def tile_gated_inverted_bottleneck_f3_kernel(
             )
             return par
 
-        be_up = keep.tile([P, G, 4], F32, name="be_up")
-        be_dn = keep.tile([P, G, 4], F32, name="be_dn")
+        be_3 = keep.tile([P, G, 4], F32, name="be_3")
+        lam_6 = keep.tile([P, G, 4], F32, name="lam_6")
 
         u_codes = keep.tile([P, B * S], U32, name="u_codes", align_bytes=64)
         u_scales = keep.tile([P, B * S], U8, name="u_scales", align_bytes=64)
@@ -194,10 +194,9 @@ def tile_gated_inverted_bottleneck_f3_kernel(
 
         e_ps = {}
         r_sb = {}
-        c_sb = {}
         a_sb = {}
         ms_sb = {}
-        z_sb = {}
+        sg_sb = {}
         gate_sb = {}
         h_sb = {}
         hq = {}
@@ -215,35 +214,31 @@ def tile_gated_inverted_bottleneck_f3_kernel(
             )
             e_ps[T] = bank
 
-        def on_scalar(T):
-            return T % 4 == 2
-
         def ramp(T):
             i, t = divmod(T, 4)
             g = i % G
-            r = work.tile([P, HALF], F32, name="r", tag="r", bufs=4)
-            if on_scalar(T):
-                nc.scalar.activation(out=r[:], in_=e_ps[T][:], func=ACT.Relu, scale=-1.0 / 6.0, bias=be_dn[:, g, t : t + 1])
-            else:
-                nc.scalar.activation(out=r[:], in_=e_ps[T][:], func=ACT.Relu, scale=1.0 / 6.0, bias=be_up[:, g, t : t + 1])
-            r_sb[T] = r
-
-        def clip(T):
-            c = work.tile([P, HALF], F32, name="c", tag="c", bufs=4)
-            if on_scalar(T):
-                nc.scalar.activation(out=c[:], in_=r_sb[T][:], func=ACT.Relu, scale=-1.0, bias=one[:])
-            else:
-                nc.vector.tensor_scalar(out=c[:], in0=r_sb[T][:], scalar1=1.0, scalar2=None, op0=ALU.min)
-            c_sb[T] = c
-
-        def swish(T):
-            i, t = divmod(T, 4)
             if t == 0:
+                r = work.tile([P, 4, HALF], F32, name="r", tag="r")
                 a = work.tile([P, 4, HALF], F32, name="a", tag="a", bufs=3)
+                r_sb[i] = r
                 a_sb[i] = a
+            nc.scalar.activation(out=r_sb[i][:, t, :], in_=e_ps[T][:], func=ACT.Relu, bias=be_3[:, g, t : t + 1])
+            if t == 3:
+                nc.scalar.activation(
+                    out=a_sb[i][:, t, :], in_=e_ps[T][:], func=ACT.Identity, bias=par_first[:, ROW_BE + g, t : t + 1]
+                )
+
+        def shift(i, q):
+            tiles = slice(0, 2) if q == 0 else slice(2, 3)
+            nc.vector.tensor_scalar(
+                out=a_sb[i][:, tiles, :], in0=r_sb[i][:, tiles, :], scalar1=3.0, scalar2=None, op0=ALU.subtract
+            )
+
+        def swish(i, q):
+            tiles = slice(2 * q, 2 * q + 2)
+            a = a_sb[i][:, tiles, :]
             nc.vector.scalar_tensor_tensor(
-                out=a_sb[i][:, t, :], in0=e_ps[T][:], scalar=par_first[:, ROW_BE + i % G, t : t + 1], in1=c_sb[T][:],
-                op0=ALU.add, op1=ALU.mult,
+                out=a, in0=r_sb[i][:, tiles, :], scalar=6.0, in1=a, op0=ALU.min, op1=ALU.mult
             )
 
         def square(T):
@@ -254,27 +249,29 @@ def tile_gated_inverted_bottleneck_f3_kernel(
             for b in range(2):
                 junk = work.tile([P, S], F32, name="junk", tag="junk")
                 nc.scalar.activation(
-                    out=junk[:], in_=a_sb[i][:, t, S * b : S * b + S], func=ACT.Square, scale=1.0 / 16.0,
+                    out=junk[:], in_=a_sb[i][:, t, S * b : S * b + S], func=ACT.Square, scale=1.0 / 96.0,
                     accum_out=ms_sb[i][:, b, t : t + 1],
                 )
 
-        def over_images(row, i):
-            return par_later[:, row + i % G, :].unsqueeze(1).to_broadcast([P, 2, 4])
+        def root(i):
+            en = work.tile([P, 2, 4], F32, name="en", tag="en")
+            nc.gpsimd.tensor_tensor(out=en[:], in0=ms_sb[i][:], in1=half_exp[:].rearrange("p (b t) -> p b t", t=4), op=ALU.pow)
+            ms_sb[i] = en
 
-        def gate_in(i):
-            z = work.tile([P, 2, 4], F32, name="z", tag="z")
-            z1 = work.tile([P, 2, 4], F32, name="z1", tag="z1")
-            z2 = work.tile([P, 2, 4], F32, name="z2", tag="z2")
-            nc.gpsimd.tensor_tensor(out=z[:], in0=ms_sb[i][:], in1=half_exp[:].rearrange("p (b t) -> p b t", t=4), op=ALU.pow)
-            nc.gpsimd.tensor_tensor(out=z1[:], in0=z[:], in1=over_images(ROW_ALPHA, i), op=ALU.mult)
-            nc.gpsimd.tensor_tensor(out=z2[:], in0=z1[:], in1=over_images(ROW_BETA, i), op=ALU.add)
-            z_sb[i] = z2
-
-        def gate_out(i):
+        def sigmoid(i):
+            g = i % G
             sg = work.tile([P, 2, 4], F32, name="sg", tag="sg")
+            for t in range(4):
+                nc.scalar.activation(
+                    out=sg[:, :, t], in_=ms_sb[i][:, :, t], func=ACT.Sigmoid,
+                    scale=par_later[:, ROW_ALPHA + g, t : t + 1], bias=par_later[:, ROW_BETA + g, t : t + 1],
+                )
+            sg_sb[i] = sg
+
+        def gate_mul(i):
             gate = work.tile([P, 2, 4], F32, name="gate", tag="gate")
-            nc.scalar.activation(out=sg[:], in_=z_sb[i][:], func=ACT.Sigmoid)
-            nc.gpsimd.tensor_tensor(out=gate[:], in0=sg[:], in1=over_images(ROW_LAM, i), op=ALU.mult)
+            lam_i = lam_6[:, i % G, :].unsqueeze(1).to_broadcast([P, 2, 4])
+            nc.vector.tensor_tensor(out=gate[:], in0=sg_sb[i][:], in1=lam_i, op=ALU.mult)
             gate_sb[i] = gate
 
         def gated(i, b):
@@ -282,9 +279,9 @@ def tile_gated_inverted_bottleneck_f3_kernel(
                 h = work.tile([P, 2, S, 4], BF16, name="h", tag="h", align_bytes=64)
                 h_sb[i] = h
             nc.vector.tensor_tensor(
-                out=h_sb[i][:, b],
-                in0=a_sb[i][:, :, S * b : S * b + S].rearrange("p t n -> p n t"),
-                in1=gate_sb[i][:, b, :].unsqueeze(1).to_broadcast([P, S, 4]),
+                out=h_sb[i][:, b].rearrange("p (c k) t -> p c t k", k=4),
+                in0=a_sb[i][:, :, S * b : S * b + S].rearrange("p t (c k) -> p c t k", k=4),
+                in1=gate_sb[i][:, b, :].unsqueeze(1).unsqueeze(3).to_broadcast([P, S // 4, 4, 4]),
                 op=ALU.mult,
             )
 
@@ -330,42 +327,51 @@ def tile_gated_inverted_bottleneck_f3_kernel(
         weight_pe("we", 0, 0)
         weight_pe("we", 0, 1)
         be_par = par_first[:, ROW_BE : ROW_BE + G, :]
-        nc.vector.tensor_scalar(out=be_up[:], in0=be_par, scalar1=1.0 / 6.0, scalar2=0.5, op0=ALU.mult, op1=ALU.add)
-        nc.vector.tensor_scalar(out=be_dn[:], in0=be_par, scalar1=-1.0 / 6.0, scalar2=0.5, op0=ALU.mult, op1=ALU.add)
+        nc.vector.tensor_scalar(out=be_3[:], in0=be_par, scalar1=3.0, scalar2=None, op0=ALU.add)
         u_interleave(0)
         we_quantize(0)
         u_quantize(0)
 
-        for s in range(-2, TILES + 8):
+        expand(0)
+        for s in range(TILES + 12):
             i, t = divmod(s, 4)
-            if s + 2 < TILES:
-                expand(s + 2)
-            if t == 1 and 0 <= i - 2 < UNITS:
-                project(i - 2)
+            if s + 1 < TILES:
+                expand(s + 1)
+            if t == 1 and 0 <= i - 3 < UNITS:
+                project(i - 3)
             if s == 0:
                 x_transposes(1)
             if s == 1:
                 par_later = transposed_rows(rows_later, ROWS_LATER, "par_later")
+                nc.vector.tensor_scalar(
+                    out=lam_6[:], in0=par_later[:, ROW_LAM : ROW_LAM + G, :], scalar1=1.0 / 6.0, scalar2=None, op0=ALU.mult
+                )
                 bp_ps = accp.tile([P, C], F32, name="bp_ps", tag="acc")
                 picked = ident_b[:, ROW_BP : ROW_BP + 1].to_broadcast([P, P])
                 nc.tensor.matmul(bp_ps[:], lhsT=picked, rhs=rows_later[:], start=True, stop=True)
                 nc.scalar.copy(out=bp_all[:], in_=bp_ps[:])
-            if 0 <= s - 1 < TILES:
-                square(s - 1)
-            if s + 2 < TILES:
-                ramp(s + 2)
+            if s < TILES:
+                ramp(s)
+            if 0 <= s - 4 < TILES:
+                square(s - 4)
+            if t == 3 and 0 <= i - 1 < UNITS:
+                root(i - 1)
+            if t == 0 and 0 <= i - 2 < UNITS:
+                sigmoid(i - 2)
+            if t == 3 and i + 2 < G:
+                weight_pe("we", i + 2, 0)
+            if t == 0 and 0 < i + 1 < G:
+                if i == 0:
+                    weight_pe("we", 1, 0)
+                weight_pe("we", i + 1, 1)
+            if t == 2 and i < G:
+                weight_pe("wp", i, 0)
             if t == 0 and 0 <= i - 1 < UNITS:
-                gate_in(i - 1)
-            if t == 1 and 0 <= i - 1 < UNITS:
-                gate_out(i - 1)
-            if t == 2 and 0 <= i < 8:
-                nc.gpsimd.tensor_tensor(out=xb[:, i, :], in0=x_sb[i // 2][:, i % 2, :], in1=bp_all[:], op=ALU.add)
-            if 0 <= s < TILES:
-                swish(s)
-            if 0 <= s + 1 < TILES:
-                clip(s + 1)
-            if t == 0 and 0 <= i - 2 < LAST:
-                h_quantize(i - 2, 0, 2)
+                shift(i - 1, 1)
+            if t == 2 and i < UNITS:
+                shift(i, 0)
+            if t == 0 and 0 <= i - 3 < LAST:
+                h_quantize(i - 3, 0, 2)
             if t == 0 and i < G:
                 wp_vector(i)
             if t == 1 and i == 0:
@@ -377,29 +383,32 @@ def tile_gated_inverted_bottleneck_f3_kernel(
                 u_interleave(1)
             if t == 3 and i == 0:
                 u_quantize(1)
-            if t == 3 and 0 < i + 2 < G:
-                weight_pe("we", i + 2, 0)
-            if t == 0 and 0 < i + 1 < G:
-                weight_pe("we", i + 1, 1)
-            if t == 2 and 0 <= i < G:
-                weight_pe("wp", i, 0)
             if t == 1 and 0 <= i - 1 < G:
                 wp_quantize(i - 1)
             if t == 1 and 0 < i + 1 < G:
                 we_quantize(i + 1)
-            if t == 2 and 0 <= i - 1 < UNITS:
-                gated(i - 1, 0)
-            if t == 3 and 0 <= i - 1 < UNITS:
-                gated(i - 1, 1)
-                if i - 1 == LAST:
+            if t == 1 and 0 <= i - 1 < UNITS:
+                swish(i - 1, 1)
+            if t == 3 and i < UNITS:
+                swish(i, 0)
+            if t == 1 and 0 <= i - 2 < UNITS:
+                gate_mul(i - 2)
+            if t == 2 and 0 <= i - 2 < UNITS:
+                gated(i - 2, 0)
+            if t == 3 and 0 <= i - 2 < UNITS:
+                gated(i - 2, 1)
+                if i - 2 == LAST:
                     h_quantize(LAST, 0, 1)
-            if t == 0 and i - 2 == LAST:
+            if t == 0 and i - 3 == LAST:
                 h_quantize(LAST, 1, 2)
-            if (i, t) == (7, 2):
+            if i == 1:
+                for j in (2 * t, 2 * t + 1):
+                    nc.vector.tensor_tensor(out=xb[:, j, :], in0=x_sb[j // 2][:, j % 2, :], in1=bp_all[:], op=ALU.add)
+            if (i, t) == (8, 2):
                 finish(0, 0)
-            if (i, t) == (7, 3):
+            if (i, t) == (8, 3):
                 finish(0, 1)
-            if (i, t) == (8, 0):
+            if (i, t) == (9, 0):
                 finish(0, 2)
                 finish(0, 3)
         for j in range(4):

@@ -10,6 +10,7 @@ F32 = mybir.dt.float32
 BF16 = mybir.dt.bfloat16
 U32 = mybir.dt.uint32
 U8 = mybir.dt.uint8
+I32 = mybir.dt.int32
 E4X4 = mybir.dt.float8_e4m3fn_x4
 E5X4 = mybir.dt.float8_e5m2_x4
 ALU = mybir.AluOpType
@@ -21,6 +22,27 @@ HALF = 512
 UNITS = 2 * G
 TILES = 4 * UNITS
 LAST = UNITS - 1
+SEED = 0x5F3759DF
+R_BUFS = 2
+A_BUFS = 6
+AFF_S = False
+WP_PE = (0, 0, 0, 1, 1, 1)
+SQ_LAG = 7
+X_LAG = 4
+CHAIN = 6
+CHAIN_LAST = 3
+H_STEP = 2
+XB_STEP = 8
+BATCHES = [(0, 1), (2, 3), (4, 5), (6, 7), (8, 9), (10, 11)]
+batch_of = {i: bt for bt in BATCHES for i in bt}
+
+
+def n_ident(i):
+    return (0 if i < 4 else 1 + i % 2)
+
+
+def PREP(s):
+    return (3 if s < 4 else 1)
 
 ROW_GAIN, ROW_BIAS, ROW_BE, ROWS_FIRST = 0, 1, 2, 8
 ROW_ALPHA, ROW_BETA, ROW_LAM, ROW_BP, ROWS_LATER = 0, 6, 12, 18, 18
@@ -43,8 +65,6 @@ def tile_gated_inverted_bottleneck_f3_kernel(
         nc.vector.memset(rows_later[:], 0.0)
         ident_f = keep.tile([P, P], F32, name="ident_f")
         ident_b = keep.tile([P, P], BF16, name="ident_b")
-        half_exp = keep.tile([P, 8], F32, name="half_exp")
-        nc.gpsimd.memset(half_exp[:], 0.5)
         one = keep.tile([P, 1], F32, name="one")
         nc.gpsimd.memset(one[:], 1.0)
         make_identity(nc, ident_f[:])
@@ -71,12 +91,12 @@ def tile_gated_inverted_bottleneck_f3_kernel(
             x_sb.append(t)
 
         def load_we(g):
-            t = keep.tile([P, 4, 512], BF16, name="we_raw%d" % g)
+            t = work.tile([P, 4, 512], BF16, name="we_raw_t", tag="we_raw", bufs=4)
             nc.sync.dma_start(out=t[:], in_=we_view[:, :, 512 * g : 512 * g + 512])
             we_raw.append(t)
 
         def load_wp(g):
-            t = keep.tile([P, 4, C], BF16, name="wp_raw%d" % g)
+            t = work.tile([P, 4, C], BF16, name="wp_raw_t", tag="wp_raw", bufs=4)
             nc.sync.dma_start(out=t[:], in_=wp_view[g])
             wp_raw.append(t)
 
@@ -110,6 +130,7 @@ def tile_gated_inverted_bottleneck_f3_kernel(
 
         be_3 = keep.tile([P, G, 4], F32, name="be_3")
         lam_6 = keep.tile([P, G, 4], F32, name="lam_6")
+        alpha_s = keep.tile([P, G, 4], F32, name="alpha_s")
 
         u_codes = keep.tile([P, B * S], U32, name="u_codes", align_bytes=64)
         u_scales = keep.tile([P, B * S], U8, name="u_scales", align_bytes=64)
@@ -141,7 +162,7 @@ def tile_gated_inverted_bottleneck_f3_kernel(
             dst = ut[n][:, t, :]
             gain = par_first[:, ROW_GAIN, t : t + 1]
             bias = par_first[:, ROW_BIAS, t : t + 1]
-            if u == 1:
+            if u == 1 or (AFF_S and n == 1):
                 nc.scalar.activation(out=dst, in_=src, func=ACT.Identity, scale=gain, bias=bias)
             else:
                 nc.vector.tensor_scalar(out=dst, in0=src, scalar1=gain, scalar2=bias, op0=ALU.mult, op1=ALU.add)
@@ -179,23 +200,28 @@ def tile_gated_inverted_bottleneck_f3_kernel(
                 nc.tensor.matmul(bank[:, o : o + 512], lhsT=ident_b[:], rhs=view, start=True, stop=True)
             nc.scalar.copy(out=wi_tile(kind, g)[:, 1024 * h : 1024 * h + 1024], in_=bank[:])
 
-        def wp_vector(g):
+        def wp_vector(g, h):
             nc.vector.tensor_copy(
-                out=wi_tile("wp", g)[:, 1024:].rearrange("p (c i j) -> p c j i", i=4, j=4),
-                in_=wp_raw[g][:, :, 256:].rearrange("p j (c i) -> p c j i", i=4),
+                out=wi_tile("wp", g)[:, 1024 * h : 1024 * h + 1024].rearrange("p (c i j) -> p c j i", i=4, j=4),
+                in_=wp_raw[g][:, :, 256 * h : 256 * h + 256].rearrange("p j (c i) -> p c j i", i=4),
             )
+            tick()
 
         def we_quantize(g):
             cols = slice(512 * g, 512 * g + 512)
             nc.vector.quantize_mx(out=we_codes[:, cols].bitcast(E4X4), scales=we_scales[:, cols], in_=wi["we", g][:])
+            tick()
 
         def wp_quantize(g):
             nc.vector.quantize_mx(out=wp_codes[:, g, :].bitcast(E4X4), scales=wp_scales[:, g, :], in_=wi["wp", g][:])
+            tick()
 
         e_ps = {}
         r_sb = {}
         a_sb = {}
         ms_sb = {}
+        en_sb = {}
+        chains = {}
         sg_sb = {}
         gate_sb = {}
         h_sb = {}
@@ -218,21 +244,21 @@ def tile_gated_inverted_bottleneck_f3_kernel(
             i, t = divmod(T, 4)
             g = i % G
             if t == 0:
-                r = work.tile([P, 4, HALF], F32, name="r", tag="r")
-                a = work.tile([P, 4, HALF], F32, name="a", tag="a", bufs=3)
+                r = work.tile([P, 4, HALF], F32, name="r", tag="r", bufs=R_BUFS)
+                a = work.tile([P, 4, HALF], F32, name="a", tag="a", bufs=A_BUFS)
                 r_sb[i] = r
                 a_sb[i] = a
             nc.scalar.activation(out=r_sb[i][:, t, :], in_=e_ps[T][:], func=ACT.Relu, bias=be_3[:, g, t : t + 1])
-            if t == 3:
+            if t >= 4 - n_ident(i):
                 nc.scalar.activation(
                     out=a_sb[i][:, t, :], in_=e_ps[T][:], func=ACT.Identity, bias=par_first[:, ROW_BE + g, t : t + 1]
                 )
 
-        def shift(i, q):
-            tiles = slice(0, 2) if q == 0 else slice(2, 3)
+        def shift(i):
             nc.vector.tensor_scalar(
-                out=a_sb[i][:, tiles, :], in0=r_sb[i][:, tiles, :], scalar1=3.0, scalar2=None, op0=ALU.subtract
+                out=a_sb[i][:, : 4 - n_ident(i), :], in0=r_sb[i][:, : 4 - n_ident(i), :], scalar1=3.0, scalar2=None, op0=ALU.subtract
             )
+            tick()
 
         def swish(i, q):
             tiles = slice(2 * q, 2 * q + 2)
@@ -240,36 +266,69 @@ def tile_gated_inverted_bottleneck_f3_kernel(
             nc.vector.scalar_tensor_tensor(
                 out=a, in0=r_sb[i][:, tiles, :], scalar=6.0, in1=a, op0=ALU.min, op1=ALU.mult
             )
+            tick()
 
         def square(T):
             i, t = divmod(T, 4)
-            if t == 0:
-                ms = work.tile([P, 2, 4], F32, name="ms", tag="ms")
+            if t == 0 and i == batch_of[i][0]:
+                ms = work.tile([P, len(batch_of[i]), 2, 4], F32, name="ms", tag="ms", bufs=3)
                 ms_sb[i] = ms
             for b in range(2):
                 junk = work.tile([P, S], F32, name="junk", tag="junk")
                 nc.scalar.activation(
                     out=junk[:], in_=a_sb[i][:, t, S * b : S * b + S], func=ACT.Square, scale=1.0 / 96.0,
-                    accum_out=ms_sb[i][:, b, t : t + 1],
+                    accum_out=ms_sb[batch_of[i][0]][:, i - batch_of[i][0], b, t : t + 1],
                 )
 
-        def root(i):
-            en = work.tile([P, 2, 4], F32, name="en", tag="en")
-            nc.gpsimd.tensor_tensor(out=en[:], in0=ms_sb[i][:], in1=half_exp[:].rearrange("p (b t) -> p b t", t=4), op=ALU.pow)
-            ms_sb[i] = en
+        def root(bt):
+            x = ms_sb[bt[0]]
+            y = [work.tile([P, len(bt), 2, 4], F32, name="y%d" % k, tag="y%d" % k, bufs=2) for k in range(3)]
+            w = work.tile([P, len(bt), 2, 4], F32, name="w", tag="w", bufs=2)
+            en = work.tile([P, len(bt), 2, 4], F32, name="en", tag="en", bufs=2)
+            ops = [
+                lambda: nc.vector.tensor_scalar(
+                    out=y[0][:].bitcast(I32), in0=x[:].bitcast(I32), scalar1=-0.5, scalar2=float(SEED), op0=ALU.mult, op1=ALU.add
+                )
+            ]
+            for k, scale in ((0, 1.0), (1, 9.0 / 64.0)):
+                ops += [
+                    lambda k=k: nc.vector.tensor_tensor(out=w[:], in0=x[:], in1=y[k][:], op=ALU.mult),
+                    lambda k=k, scale=scale: nc.vector.scalar_tensor_tensor(
+                        out=w[:], in0=w[:], scalar=scale, in1=y[k][:], op0=ALU.mult, op1=ALU.mult
+                    ),
+                    lambda: nc.vector.scalar_tensor_tensor(
+                        out=w[:], in0=w[:], scalar=-10.0 / 3.0, in1=w[:], op0=ALU.add, op1=ALU.mult
+                    ),
+                    lambda k=k: nc.vector.scalar_tensor_tensor(
+                        out=y[k + 1][:], in0=w[:], scalar=5.0, in1=y[k][:], op0=ALU.add, op1=ALU.mult
+                    ),
+                ]
+            ops.append(lambda: nc.vector.tensor_tensor(out=en[:], in0=x[:], in1=y[2][:], op=ALU.mult))
+            chains[bt] = ops
+            en_sb[bt[0]] = en
+
+        def tick():
+            for ops in chains.values():
+                if ops:
+                    ops.pop(0)()
+
+        def finish_root(bt):
+            for op in chains.pop(bt):
+                op()
 
         def sigmoid(i):
             g = i % G
-            sg = work.tile([P, 2, 4], F32, name="sg", tag="sg")
+            en = en_sb[batch_of[i][0]][:, i - batch_of[i][0]]
+            sg = work.tile([P, 2, 4], F32, name="sg", tag="sg", bufs=3)
             for t in range(4):
                 nc.scalar.activation(
-                    out=sg[:, :, t], in_=ms_sb[i][:, :, t], func=ACT.Sigmoid,
-                    scale=par_later[:, ROW_ALPHA + g, t : t + 1], bias=par_later[:, ROW_BETA + g, t : t + 1],
+                    out=sg[:, :, t], in_=en[:, :, t], func=ACT.Sigmoid,
+                    scale=alpha_s[:, g, t : t + 1], bias=later[0][:, ROW_BETA + g, t : t + 1],
                 )
             sg_sb[i] = sg
 
         def gate_mul(i):
-            gate = work.tile([P, 2, 4], F32, name="gate", tag="gate")
+            gate = work.tile([P, 2, 4], F32, name="gate", tag="gate", bufs=3)
             lam_i = lam_6[:, i % G, :].unsqueeze(1).to_broadcast([P, 2, 4])
             nc.vector.tensor_tensor(out=gate[:], in0=sg_sb[i][:], in1=lam_i, op=ALU.mult)
             gate_sb[i] = gate
@@ -284,6 +343,7 @@ def tile_gated_inverted_bottleneck_f3_kernel(
                 in1=gate_sb[i][:, b, :].unsqueeze(1).unsqueeze(3).to_broadcast([P, S // 4, 4, 4]),
                 op=ALU.mult,
             )
+            tick()
 
         def h_quantize(i, b0, b1):
             if b0 == 0:
@@ -296,6 +356,7 @@ def tile_gated_inverted_bottleneck_f3_kernel(
                 out=codes[:, cols].bitcast(E5X4), scales=scales[:, cols],
                 in_=h_sb[i][:].rearrange("p b n t -> p (b n t)")[:, 4 * S * b0 : 4 * S * b1],
             )
+            tick()
 
         def project(i):
             n, g = divmod(i, G)
@@ -318,6 +379,25 @@ def tile_gated_inverted_bottleneck_f3_kernel(
             nc.vector.tensor_tensor(out=o[:], in0=acc[n, j][:], in1=xb[:, 4 * n + j, :], op=ALU.add)
             nc.sync.dma_start(out=out_view[2 * n + j // 2, j % 2], in_=o[:])
 
+        later = {}
+
+        def later_parameters():
+            par = transposed_rows(rows_later, ROWS_LATER, "par_later")
+            later[0] = par
+            nc.vector.tensor_scalar(
+                out=lam_6[:], in0=par[:, ROW_LAM : ROW_LAM + G, :], scalar1=1.0 / 6.0, scalar2=None, op0=ALU.mult
+            )
+            nc.vector.tensor_scalar(
+                out=alpha_s[:], in0=par[:, ROW_ALPHA : ROW_ALPHA + G, :], scalar1=9.0 / 64.0, scalar2=None, op0=ALU.mult
+            )
+            bp_ps = accp.tile([P, C], F32, name="bp_ps", tag="acc")
+            picked = ident_b[:, ROW_BP : ROW_BP + 1].to_broadcast([P, P])
+            nc.tensor.matmul(bp_ps[:], lhsT=picked, rhs=rows_later[:], start=True, stop=True)
+            nc.scalar.copy(out=bp_all[:], in_=bp_ps[:])
+
+        def add_bias(j):
+            nc.vector.tensor_tensor(out=xb[:, j, :], in0=x_sb[j // 2][:, j % 2, :], in1=bp_all[:], op=ALU.add)
+
         x_transposes(0)
         par_first = transposed_rows(rows_first, ROWS_FIRST, "par_first")
         affine(0, 2)
@@ -332,84 +412,76 @@ def tile_gated_inverted_bottleneck_f3_kernel(
         we_quantize(0)
         u_quantize(0)
 
-        expand(0)
-        for s in range(TILES + 12):
-            i, t = divmod(s, 4)
-            if s + 1 < TILES:
-                expand(s + 1)
-            if t == 1 and 0 <= i - 3 < UNITS:
-                project(i - 3)
-            if s == 0:
-                x_transposes(1)
-            if s == 1:
-                par_later = transposed_rows(rows_later, ROWS_LATER, "par_later")
-                nc.vector.tensor_scalar(
-                    out=lam_6[:], in0=par_later[:, ROW_LAM : ROW_LAM + G, :], scalar1=1.0 / 6.0, scalar2=None, op0=ALU.mult
-                )
-                bp_ps = accp.tile([P, C], F32, name="bp_ps", tag="acc")
-                picked = ident_b[:, ROW_BP : ROW_BP + 1].to_broadcast([P, P])
-                nc.tensor.matmul(bp_ps[:], lhsT=picked, rhs=rows_later[:], start=True, stop=True)
-                nc.scalar.copy(out=bp_all[:], in_=bp_ps[:])
-            if s < TILES:
-                ramp(s)
-            if 0 <= s - 4 < TILES:
-                square(s - 4)
-            if t == 3 and 0 <= i - 1 < UNITS:
-                root(i - 1)
-            if t == 0 and 0 <= i - 2 < UNITS:
-                sigmoid(i - 2)
-            if t == 3 and i + 2 < G:
-                weight_pe("we", i + 2, 0)
-            if t == 0 and 0 < i + 1 < G:
-                if i == 0:
-                    weight_pe("we", 1, 0)
-                weight_pe("we", i + 1, 1)
-            if t == 2 and i < G:
-                weight_pe("wp", i, 0)
-            if t == 0 and 0 <= i - 1 < UNITS:
-                shift(i - 1, 1)
-            if t == 2 and i < UNITS:
-                shift(i, 0)
-            if t == 0 and 0 <= i - 3 < LAST:
-                h_quantize(i - 3, 0, 2)
-            if t == 0 and i < G:
-                wp_vector(i)
-            if t == 1 and i == 0:
-                affine(1, 2)
-                affine(1, 0)
-                affine(1, 3)
-                affine(1, 1)
-            if t == 2 and i == 0:
-                u_interleave(1)
-            if t == 3 and i == 0:
-                u_quantize(1)
-            if t == 1 and 0 <= i - 1 < G:
-                wp_quantize(i - 1)
-            if t == 1 and 0 < i + 1 < G:
-                we_quantize(i + 1)
-            if t == 1 and 0 <= i - 1 < UNITS:
-                swish(i - 1, 1)
-            if t == 3 and i < UNITS:
-                swish(i, 0)
-            if t == 1 and 0 <= i - 2 < UNITS:
-                gate_mul(i - 2)
-            if t == 2 and 0 <= i - 2 < UNITS:
-                gated(i - 2, 0)
-            if t == 3 and 0 <= i - 2 < UNITS:
-                gated(i - 2, 1)
-                if i - 2 == LAST:
-                    h_quantize(LAST, 0, 1)
-            if t == 0 and i - 3 == LAST:
-                h_quantize(LAST, 1, 2)
-            if i == 1:
-                for j in (2 * t, 2 * t + 1):
-                    nc.vector.tensor_tensor(out=xb[:, j, :], in0=x_sb[j // 2][:, j % 2, :], in1=bp_all[:], op=ALU.add)
-            if (i, t) == (8, 2):
-                finish(0, 0)
-            if (i, t) == (8, 3):
-                finish(0, 1)
-            if (i, t) == (9, 0):
-                finish(0, 2)
-                finish(0, 3)
+        prep = []
+        for g in range(1, G + 1):
+            if g < G:
+                prep.append(lambda g=g: weight_pe("we", g, 0))
+                prep.append(lambda g=g: weight_pe("we", g, 1))
+            for h in range(2):
+                if h < WP_PE[g - 1]:
+                    prep.append(lambda g=g, h=h: weight_pe("wp", g - 1, h))
+                else:
+                    prep.append(lambda g=g, h=h: wp_vector(g - 1, h))
+            if g < G:
+                prep.append(lambda g=g: we_quantize(g))
+            prep.append(lambda g=g: wp_quantize(g - 1))
+
+        at = {}
+
+        def plan(step, phase, fn, *args):
+            at.setdefault((step, phase), []).append((fn, args))
+
+        for s in range(TILES):
+            plan(s - 1, "T0", expand, s)
+            plan(s, "S0", ramp, s)
+            plan(s + SQ_LAG, "S1", square, s)
+        for i in range(UNITS):
+            plan(4 * i + X_LAG, "V0", shift, i)
+            plan(4 * i + X_LAG + 1, "V1", swish, i, 0)
+            plan(4 * i + X_LAG + 2, "V1", swish, i, 1)
+        last_h = -1
+        finished = {}
+        for bt in BATCHES:
+            c0 = 4 * bt[-1] + SQ_LAG + 4
+            w = CHAIN if bt[-1] < UNITS - 1 else CHAIN_LAST
+            plan(c0 - 1, "V9", root, bt)
+            plan(c0 + w - 1, "V9", finish_root, bt)
+            h0 = max(c0 + w + 1, last_h)
+            for i in bt:
+                plan(c0 + w, "S2", sigmoid, i)
+                plan(h0 - 1, "V8", gate_mul, i)
+                plan(h0, "V5", gated, i, 0)
+                plan(h0 + 1, "V5", gated, i, 1)
+                if i == LAST:
+                    plan(h0 + 1, "V6", h_quantize, i, 0, 1)
+                    plan(h0 + 2, "V6", h_quantize, i, 1, 2)
+                else:
+                    plan(h0 + 2, "V6", h_quantize, i, 0, 2)
+                plan(h0 + 4, "T1", project, i)
+                finished[i] = h0 + 4
+                h0 += H_STEP
+            last_h = h0
+        for j in range(4):
+            plan(finished[G - 1] + 1 + j // 2, "V7", finish, 0, j)
+        assert finished[G] > finished[G - 1] + 2
+        for j in range(8):
+            plan(XB_STEP + j, "V4", add_bias, j)
+        plan(0, "T2", x_transposes, 1)
+        for t in range(4):
+            plan(1, "V3", affine, 1, t)
+        plan(2, "V3", u_interleave, 1)
+        plan(3, "V3", u_quantize, 1)
+        plan(5, "T2", later_parameters)
+
+        for s in range(-1, finished[LAST] + 1):
+            for phase in ("T0", "T1", "T2", "S0", "S1", "S2", "V0", "V1"):
+                for fn, args in at.get((s, phase), []):
+                    fn(*args)
+            for event in prep[: PREP(s)]:
+                event()
+                prep.pop(0)
+            for phase in ("V3", "V4", "V5", "V6", "V7", "V8", "V9"):
+                for fn, args in at.get((s, phase), []):
+                    fn(*args)
         for j in range(4):
             finish(1, j)

@@ -23,26 +23,35 @@ UNITS = 2 * G
 TILES = 4 * UNITS
 LAST = UNITS - 1
 SEED = 0x5F3759DF
-R_BUFS = 2
+BANKS = 5
+R_BUFS = 4
 A_BUFS = 6
-AFF_S = False
-WP_PE = (0, 0, 0, 1, 1, 1)
-SQ_LAG = 7
-X_LAG = 4
-CHAIN = 6
-CHAIN_LAST = 3
-H_STEP = 2
-XB_STEP = 8
+WP = ('VV', 'PV', 'PP', 'PV', 'PP', 'PP')
+WE = ('PP', 'VV', 'PP', 'VV', 'PV', 'PP')
+SQ_LAG = 2
+CHAIN_OPS = 3
+XB_STEP = 4
+XB_GAP = 2
+XB = 'VVVVVVVG'
+X1_STEP = -2
+LATER_STEP = 0
+HQ_BUFS = 7
+RAMP_LEAD = 2
+SG_GAP = 1
+GATE_GAP = 0
+AFF_S = ()
+SG = (7, 10, 11)
+PHASES = ('T0', 'T1', 'T2', 'T3', 'S0', 'S1', 'S2', 'G0', 'G1', 'G2', 'V0', 'V1', 'V3', 'V2')
 BATCHES = [(0, 1), (2, 3), (4, 5), (6, 7), (8, 9), (10, 11)]
 batch_of = {i: bt for bt in BATCHES for i in bt}
 
 
-def n_ident(i):
-    return (0 if i < 4 else 1 + i % 2)
-
-
 def PREP(s):
     return (3 if s < 4 else 1)
+
+
+def CLIP_V(T):
+    return False
 
 ROW_GAIN, ROW_BIAS, ROW_BE, ROWS_FIRST = 0, 1, 2, 8
 ROW_ALPHA, ROW_BETA, ROW_LAM, ROW_BP, ROWS_LATER = 0, 6, 12, 18, 18
@@ -55,8 +64,9 @@ def tile_gated_inverted_bottleneck_f3_kernel(
     with ExitStack() as ctx:
         keep = ctx.enter_context(tc.tile_pool(name="keep", bufs=1))
         work = ctx.enter_context(tc.tile_pool(name="work", bufs=2))
-        bankp = ctx.enter_context(tc.psum_pool(name="bankp", bufs=4))
-        accp = ctx.enter_context(tc.psum_pool(name="accp", bufs=4))
+        bankp = ctx.enter_context(tc.psum_pool(name="bankp", bufs=BANKS))
+        accp = ctx.enter_context(tc.psum_pool(name="accp", bufs=7 - BANKS))
+        gatep = ctx.enter_context(tc.psum_pool(name="gatep", bufs=1))
         ctx.enter_context(tc.manual_schedule())
 
         rows_first = keep.tile([P, C], BF16, name="rows_first")
@@ -128,9 +138,7 @@ def tile_gated_inverted_bottleneck_f3_kernel(
             )
             return par
 
-        be_3 = keep.tile([P, G, 4], F32, name="be_3")
-        lam_6 = keep.tile([P, G, 4], F32, name="lam_6")
-        alpha_s = keep.tile([P, G, 4], F32, name="alpha_s")
+        be_c = keep.tile([P, G, 4], F32, name="be_c")
 
         u_codes = keep.tile([P, B * S], U32, name="u_codes", align_bytes=64)
         u_scales = keep.tile([P, B * S], U8, name="u_scales", align_bytes=64)
@@ -146,7 +154,7 @@ def tile_gated_inverted_bottleneck_f3_kernel(
 
         def x_transposes(n):
             for u in range(2):
-                t = accp.tile([P, HALF], F32, name="xt", tag="acc")
+                t = (bankp if n == 0 else accp).tile([P, HALF], F32, name="xt", tag="bank" if n == 0 else "acc")
                 for j in range(4):
                     words = x_sb[2 * n + j // 2][:].rearrange("p i c -> p (i c)").bitcast(F32)
                     w0 = (C // 2) * (j % 2)
@@ -162,7 +170,7 @@ def tile_gated_inverted_bottleneck_f3_kernel(
             dst = ut[n][:, t, :]
             gain = par_first[:, ROW_GAIN, t : t + 1]
             bias = par_first[:, ROW_BIAS, t : t + 1]
-            if u == 1 or (AFF_S and n == 1):
+            if u == 1 or n in AFF_S:
                 nc.scalar.activation(out=dst, in_=src, func=ACT.Identity, scale=gain, bias=bias)
             else:
                 nc.vector.tensor_scalar(out=dst, in0=src, scalar1=gain, scalar2=bias, op0=ALU.mult, op1=ALU.add)
@@ -183,14 +191,14 @@ def tile_gated_inverted_bottleneck_f3_kernel(
 
         wi = {}
 
-        def wi_tile(kind, g):
+        def wi_half(kind, g, h):
             if (kind, g) not in wi:
                 t = work.tile([P, 2048], BF16, name="wi_" + kind, tag="wi_" + kind, align_bytes=64)
                 wi[kind, g] = t
-            return wi[kind, g]
+            return wi[kind, g][:, 1024 * h : 1024 * h + 1024]
 
         def weight_pe(kind, g, h):
-            bank = bankp.tile([P, 1024], BF16, name="bank", tag="bank")
+            bank = bankp.tile([P, 1024], BF16, name="bank_w", tag="bank")
             for q in (2 * h, 2 * h + 1):
                 if kind == "we":
                     view = we_raw[g][:].rearrange("p j (m t) -> p t m j", t=4)[:, q]
@@ -198,35 +206,56 @@ def tile_gated_inverted_bottleneck_f3_kernel(
                     view = wp_raw[g][:, :, P * q : P * q + P].rearrange("p j c -> p c j")
                 o = 512 * (q % 2)
                 nc.tensor.matmul(bank[:, o : o + 512], lhsT=ident_b[:], rhs=view, start=True, stop=True)
-            nc.scalar.copy(out=wi_tile(kind, g)[:, 1024 * h : 1024 * h + 1024], in_=bank[:])
+            nc.scalar.copy(out=wi_half(kind, g, h), in_=bank[:])
 
-        def wp_vector(g, h):
-            nc.vector.tensor_copy(
-                out=wi_tile("wp", g)[:, 1024 * h : 1024 * h + 1024].rearrange("p (c i j) -> p c j i", i=4, j=4),
-                in_=wp_raw[g][:, :, 256 * h : 256 * h + 256].rearrange("p j (c i) -> p c j i", i=4),
-            )
-            tick()
+        def weight_sb(kind, g, h, mode):
+            dst = wi_half(kind, g, h)
+            if kind == "we":
+                pairs = [
+                    (dst[:, 512 * k : 512 * k + 512].rearrange("p (m j) -> p m j", j=4),
+                     we_raw[g][:].rearrange("p j (m t) -> p t m j", t=4)[:, 2 * h + k]) for k in range(2)
+                ]
+            else:
+                pairs = [
+                    (dst.rearrange("p (c i j) -> p c j i", i=4, j=4),
+                     wp_raw[g][:, :, 256 * h : 256 * h + 256].rearrange("p j (c i) -> p c j i", i=4))
+                ]
+            for o, src in pairs:
+                if mode == "V":
+                    nc.vector.tensor_copy(out=o, in_=src)
+                elif mode == "S":
+                    nc.scalar.copy(out=o, in_=src)
+                else:
+                    nc.gpsimd.tensor_scalar(out=o, in0=src, scalar1=1.0, scalar2=0.0, op0=ALU.mult, op1=ALU.add)
+
+        def weight(kind, g, h, mode):
+            if mode == "P":
+                weight_pe(kind, g, h)
+            else:
+                weight_sb(kind, g, h, mode)
 
         def we_quantize(g):
             cols = slice(512 * g, 512 * g + 512)
             nc.vector.quantize_mx(out=we_codes[:, cols].bitcast(E4X4), scales=we_scales[:, cols], in_=wi["we", g][:])
-            tick()
 
         def wp_quantize(g):
             nc.vector.quantize_mx(out=wp_codes[:, g, :].bitcast(E4X4), scales=wp_scales[:, g, :], in_=wi["wp", g][:])
-            tick()
 
         e_ps = {}
         r_sb = {}
+        c_sb = {}
         a_sb = {}
         ms_sb = {}
         en_sb = {}
         chains = {}
         sg_sb = {}
         gate_sb = {}
+        gate_ps = {}
         h_sb = {}
+        hs_sb = {}
         hq = {}
         acc = {}
+        later = {}
 
         def expand(T):
             i, t = divmod(T, 4)
@@ -242,113 +271,141 @@ def tile_gated_inverted_bottleneck_f3_kernel(
 
         def ramp(T):
             i, t = divmod(T, 4)
-            g = i % G
+            r = work.tile([P, HALF], F32, name="r", tag="r", bufs=R_BUFS)
+            nc.scalar.activation(
+                out=r[:], in_=e_ps[T][:], func=ACT.Relu, scale=1.0 / 6.0, bias=be_c[:, i % G, t : t + 1]
+            )
+            r_sb[T] = r
+
+        def clip(T):
+            c = work.tile([P, HALF], F32, name="c", tag="c", bufs=R_BUFS)
+            if CLIP_V(T):
+                nc.vector.tensor_scalar(out=c[:], in0=r_sb[T][:], scalar1=1.0, scalar2=None, op0=ALU.min)
+            else:
+                nc.gpsimd.tensor_scalar(out=c[:], in0=r_sb[T][:], scalar1=1.0, scalar2=1.0, op0=ALU.min, op1=ALU.mult)
+            c_sb[T] = c
+
+        def swish(T):
+            i, t = divmod(T, 4)
             if t == 0:
-                r = work.tile([P, 4, HALF], F32, name="r", tag="r", bufs=R_BUFS)
                 a = work.tile([P, 4, HALF], F32, name="a", tag="a", bufs=A_BUFS)
-                r_sb[i] = r
                 a_sb[i] = a
-            nc.scalar.activation(out=r_sb[i][:, t, :], in_=e_ps[T][:], func=ACT.Relu, bias=be_3[:, g, t : t + 1])
-            if t >= 4 - n_ident(i):
-                nc.scalar.activation(
-                    out=a_sb[i][:, t, :], in_=e_ps[T][:], func=ACT.Identity, bias=par_first[:, ROW_BE + g, t : t + 1]
-                )
-
-        def shift(i):
-            nc.vector.tensor_scalar(
-                out=a_sb[i][:, : 4 - n_ident(i), :], in0=r_sb[i][:, : 4 - n_ident(i), :], scalar1=3.0, scalar2=None, op0=ALU.subtract
-            )
-            tick()
-
-        def swish(i, q):
-            tiles = slice(2 * q, 2 * q + 2)
-            a = a_sb[i][:, tiles, :]
             nc.vector.scalar_tensor_tensor(
-                out=a, in0=r_sb[i][:, tiles, :], scalar=6.0, in1=a, op0=ALU.min, op1=ALU.mult
+                out=a_sb[i][:, t, :], in0=e_ps[T][:], scalar=par_first[:, ROW_BE + i % G, t : t + 1], in1=c_sb[T][:],
+                op0=ALU.add, op1=ALU.mult,
             )
-            tick()
 
         def square(T):
             i, t = divmod(T, 4)
-            if t == 0 and i == batch_of[i][0]:
-                ms = work.tile([P, len(batch_of[i]), 2, 4], F32, name="ms", tag="ms", bufs=3)
-                ms_sb[i] = ms
+            bt = batch_of[i]
+            if t == 0 and i == bt[0]:
+                ms = work.tile([P, len(bt), 2, 4], F32, name="ms", tag="ms", bufs=3)
+                ms_sb[bt] = ms
             for b in range(2):
                 junk = work.tile([P, S], F32, name="junk", tag="junk")
                 nc.scalar.activation(
-                    out=junk[:], in_=a_sb[i][:, t, S * b : S * b + S], func=ACT.Square, scale=1.0 / 96.0,
-                    accum_out=ms_sb[batch_of[i][0]][:, i - batch_of[i][0], b, t : t + 1],
+                    out=junk[:], in_=a_sb[i][:, t, S * b : S * b + S], func=ACT.Square, scale=1.0 / 16.0,
+                    accum_out=ms_sb[bt][:, i - bt[0], b, t : t + 1],
                 )
 
-        def root(bt):
-            x = ms_sb[bt[0]]
-            y = [work.tile([P, len(bt), 2, 4], F32, name="y%d" % k, tag="y%d" % k, bufs=2) for k in range(3)]
-            w = work.tile([P, len(bt), 2, 4], F32, name="w", tag="w", bufs=2)
-            en = work.tile([P, len(bt), 2, 4], F32, name="en", tag="en", bufs=2)
-            ops = [
-                lambda: nc.vector.tensor_scalar(
-                    out=y[0][:].bitcast(I32), in0=x[:].bitcast(I32), scalar1=-0.5, scalar2=float(SEED), op0=ALU.mult, op1=ALU.add
+        def root_start(bt):
+            x = ms_sb[bt]
+            shape = [P, len(bt), 2, 4]
+            y = [work.tile(shape, F32, name="y%d" % k, tag="y%d" % k, bufs=2) for k in range(2)]
+            w = work.tile(shape, F32, name="w", tag="w", bufs=2)
+            v = work.tile(shape, F32, name="v", tag="v", bufs=2)
+            q = work.tile(shape, F32, name="q", tag="q", bufs=2)
+            en = work.tile(shape, F32, name="en", tag="en", bufs=2)
+            nc.vector.tensor_scalar(
+                out=y[0][:].bitcast(I32), in0=x[:].bitcast(I32), scalar1=-0.5, scalar2=float(SEED), op0=ALU.mult, op1=ALU.add
+            )
+
+            def mul(o, a, b):
+                return lambda: nc.gpsimd.tensor_tensor(out=o[:], in0=a[:], in1=b[:], op=ALU.mult)
+
+            def affine_of(o, a, m, k):
+                return lambda: nc.gpsimd.tensor_scalar(
+                    out=o[:], in0=a[:], scalar1=m, scalar2=k, op0=ALU.mult, op1=ALU.add
                 )
-            ]
-            for k, scale in ((0, 1.0), (1, 9.0 / 64.0)):
+
+            ops = []
+            for k in range(2):
                 ops += [
-                    lambda k=k: nc.vector.tensor_tensor(out=w[:], in0=x[:], in1=y[k][:], op=ALU.mult),
-                    lambda k=k, scale=scale: nc.vector.scalar_tensor_tensor(
-                        out=w[:], in0=w[:], scalar=scale, in1=y[k][:], op0=ALU.mult, op1=ALU.mult
-                    ),
-                    lambda: nc.vector.scalar_tensor_tensor(
-                        out=w[:], in0=w[:], scalar=-10.0 / 3.0, in1=w[:], op0=ALU.add, op1=ALU.mult
-                    ),
-                    lambda k=k: nc.vector.scalar_tensor_tensor(
-                        out=y[k + 1][:], in0=w[:], scalar=5.0, in1=y[k][:], op0=ALU.add, op1=ALU.mult
-                    ),
+                    mul(w, x, y[k]), mul(v, w, y[k]), affine_of(q, v, 0.375, -1.25), mul(v, q, v),
+                    affine_of(q, v, 1.0, 1.875), mul((y[1], en)[k], q, (y[0], w)[k]),
                 ]
-            ops.append(lambda: nc.vector.tensor_tensor(out=en[:], in0=x[:], in1=y[2][:], op=ALU.mult))
             chains[bt] = ops
-            en_sb[bt[0]] = en
+            en_sb[bt] = en
 
-        def tick():
-            for ops in chains.values():
-                if ops:
-                    ops.pop(0)()
-
-        def finish_root(bt):
-            for op in chains.pop(bt):
+        def root_steps(bt, last):
+            count = len(chains[bt]) if last else CHAIN_OPS
+            for op in chains[bt][:count]:
                 op()
+            chains[bt] = chains[bt][count:]
 
         def sigmoid(i):
             g = i % G
-            en = en_sb[batch_of[i][0]][:, i - batch_of[i][0]]
+            bt = batch_of[i]
+            en = en_sb[bt][:, i - bt[0]]
             sg = work.tile([P, 2, 4], F32, name="sg", tag="sg", bufs=3)
             for t in range(4):
                 nc.scalar.activation(
                     out=sg[:, :, t], in_=en[:, :, t], func=ACT.Sigmoid,
-                    scale=alpha_s[:, g, t : t + 1], bias=later[0][:, ROW_BETA + g, t : t + 1],
+                    scale=later[0][:, ROW_ALPHA + g, t : t + 1], bias=later[0][:, ROW_BETA + g, t : t + 1],
                 )
             sg_sb[i] = sg
 
         def gate_mul(i):
             gate = work.tile([P, 2, 4], F32, name="gate", tag="gate", bufs=3)
-            lam_i = lam_6[:, i % G, :].unsqueeze(1).to_broadcast([P, 2, 4])
-            nc.vector.tensor_tensor(out=gate[:], in0=sg_sb[i][:], in1=lam_i, op=ALU.mult)
+            lam_i = later[0][:, ROW_LAM + i % G, :].unsqueeze(1).to_broadcast([P, 2, 4])
+            nc.gpsimd.tensor_tensor(out=gate[:], in0=sg_sb[i][:], in1=lam_i, op=ALU.mult)
             gate_sb[i] = gate
 
-        def gated(i, b):
+        gates = gatep.tile([P, UNITS, 2, 4], F32, name="gates")
+
+        def gate_move(i):
+            nc.tensor.matmul(
+                gates[:, i].rearrange("p b t -> p (b t)"), lhsT=ident_f[:],
+                rhs=gate_sb[i][:].rearrange("p b t -> p (b t)"), start=True, stop=True,
+            )
+
+        def gated(i, q):
+            b, part = divmod(q, 2)
+            if q == 0:
+                h = work.tile([P, 2, S, 4], BF16, name="h", tag="h", align_bytes=64)
+                h_sb[i] = h
+            n0 = P * part
+            nc.vector.tensor_tensor(
+                out=h_sb[i][:, b, n0 : n0 + P].rearrange("p (c k) t -> p c t k", k=4),
+                in0=a_sb[i][:, :, S * b + n0 : S * b + n0 + P].rearrange("p t (c k) -> p c t k", k=4),
+                in1=gates[:, i, b, :].unsqueeze(1).unsqueeze(3).to_broadcast([P, P // 4, 4, 4]),
+                op=ALU.mult,
+            )
+
+        def gated_scalar(i, q):
+            b, part = divmod(q, 2)
+            if q == 0:
+                hs = work.tile([P, 4, HALF], BF16, name="hs", tag="hs", bufs=1)
+                hs_sb[i] = hs
+            for t in (2 * part, 2 * part + 1):
+                cols = slice(S * b, S * b + S)
+                nc.scalar.activation(
+                    out=hs_sb[i][:, t, cols], in_=a_sb[i][:, t, cols], func=ACT.Copy, scale=gate_sb[i][:, b, t : t + 1]
+                )
+
+        def gather(i, b):
             if b == 0:
                 h = work.tile([P, 2, S, 4], BF16, name="h", tag="h", align_bytes=64)
                 h_sb[i] = h
-            nc.vector.tensor_tensor(
+            nc.vector.tensor_copy(
                 out=h_sb[i][:, b].rearrange("p (c k) t -> p c t k", k=4),
-                in0=a_sb[i][:, :, S * b : S * b + S].rearrange("p t (c k) -> p c t k", k=4),
-                in1=gate_sb[i][:, b, :].unsqueeze(1).unsqueeze(3).to_broadcast([P, S // 4, 4, 4]),
-                op=ALU.mult,
+                in_=hs_sb[i][:, :, S * b : S * b + S].rearrange("p t (c k) -> p c t k", k=4),
             )
-            tick()
 
         def h_quantize(i, b0, b1):
             if b0 == 0:
-                codes = work.tile([P, HALF], U32, name="h_codes", tag="h_codes", align_bytes=64)
-                scales = work.tile([P, HALF], U8, name="h_scales", tag="h_scales", align_bytes=64)
+                codes = work.tile([P, HALF], U32, name="h_codes", tag="h_codes", align_bytes=64, bufs=HQ_BUFS)
+                scales = work.tile([P, HALF], U8, name="h_scales", tag="h_scales", align_bytes=64, bufs=HQ_BUFS)
                 hq[i] = (codes, scales)
             codes, scales = hq[i]
             cols = slice(S * b0, S * b1)
@@ -356,21 +413,22 @@ def tile_gated_inverted_bottleneck_f3_kernel(
                 out=codes[:, cols].bitcast(E5X4), scales=scales[:, cols],
                 in_=h_sb[i][:].rearrange("p b n t -> p (b n t)")[:, 4 * S * b0 : 4 * S * b1],
             )
-            tick()
 
-        def project(i):
+        def project(i, j):
             n, g = divmod(i, G)
             codes, scales = hq[i]
-            for j in range(4):
-                if g == 0:
+            if g == 0:
+                if j < 7 - BANKS or n == 0:
                     t = accp.tile([P, C], F32, name="acc", tag="acc")
-                    acc[n, j] = t
-                m = slice(P * j, P * j + P)
-                nc.tensor.matmul_mx(
-                    out=acc[n, j][:], lhsT=codes[:, m].bitcast(E5X4), lhsT_scale=scales[:, m],
-                    rhs=wp_codes[:, g, :].bitcast(E4X4), rhs_scale=wp_scales[:, g, :],
-                    start=(g == 0), stop=(g == G - 1),
-                )
+                else:
+                    t = bankp.tile([P, C], F32, name="acc_b", tag="bank")
+                acc[n, j] = t
+            m = slice(P * j, P * j + P)
+            nc.tensor.matmul_mx(
+                out=acc[n, j][:], lhsT=codes[:, m].bitcast(E5X4), lhsT_scale=scales[:, m],
+                rhs=wp_codes[:, g, :].bitcast(E4X4), rhs_scale=wp_scales[:, g, :],
+                start=(g == 0), stop=(g == G - 1),
+            )
 
         out_view = out.rearrange("(b p i) c -> b i p c", p=P, i=2)
 
@@ -379,24 +437,18 @@ def tile_gated_inverted_bottleneck_f3_kernel(
             nc.vector.tensor_tensor(out=o[:], in0=acc[n, j][:], in1=xb[:, 4 * n + j, :], op=ALU.add)
             nc.sync.dma_start(out=out_view[2 * n + j // 2, j % 2], in_=o[:])
 
-        later = {}
-
         def later_parameters():
-            par = transposed_rows(rows_later, ROWS_LATER, "par_later")
-            later[0] = par
-            nc.vector.tensor_scalar(
-                out=lam_6[:], in0=par[:, ROW_LAM : ROW_LAM + G, :], scalar1=1.0 / 6.0, scalar2=None, op0=ALU.mult
-            )
-            nc.vector.tensor_scalar(
-                out=alpha_s[:], in0=par[:, ROW_ALPHA : ROW_ALPHA + G, :], scalar1=9.0 / 64.0, scalar2=None, op0=ALU.mult
-            )
+            later[0] = transposed_rows(rows_later, ROWS_LATER, "par_later")
             bp_ps = accp.tile([P, C], F32, name="bp_ps", tag="acc")
             picked = ident_b[:, ROW_BP : ROW_BP + 1].to_broadcast([P, P])
             nc.tensor.matmul(bp_ps[:], lhsT=picked, rhs=rows_later[:], start=True, stop=True)
             nc.scalar.copy(out=bp_all[:], in_=bp_ps[:])
 
         def add_bias(j):
-            nc.vector.tensor_tensor(out=xb[:, j, :], in0=x_sb[j // 2][:, j % 2, :], in1=bp_all[:], op=ALU.add)
+            if XB[j] == "G":
+                nc.gpsimd.tensor_tensor(out=xb[:, j, :], in0=x_sb[j // 2][:, j % 2, :], in1=bp_all[:], op=ALU.add)
+            else:
+                nc.vector.tensor_tensor(out=xb[:, j, :], in0=x_sb[j // 2][:, j % 2, :], in1=bp_all[:], op=ALU.add)
 
         x_transposes(0)
         par_first = transposed_rows(rows_first, ROWS_FIRST, "par_first")
@@ -404,10 +456,10 @@ def tile_gated_inverted_bottleneck_f3_kernel(
         affine(0, 0)
         affine(0, 3)
         affine(0, 1)
-        weight_pe("we", 0, 0)
-        weight_pe("we", 0, 1)
+        for h in range(2):
+            weight("we", 0, h, WE[0][h])
         be_par = par_first[:, ROW_BE : ROW_BE + G, :]
-        nc.vector.tensor_scalar(out=be_3[:], in0=be_par, scalar1=3.0, scalar2=None, op0=ALU.add)
+        nc.vector.tensor_scalar(out=be_c[:], in0=be_par, scalar1=1.0 / 6.0, scalar2=0.5, op0=ALU.mult, op1=ALU.add)
         u_interleave(0)
         we_quantize(0)
         u_quantize(0)
@@ -415,13 +467,10 @@ def tile_gated_inverted_bottleneck_f3_kernel(
         prep = []
         for g in range(1, G + 1):
             if g < G:
-                prep.append(lambda g=g: weight_pe("we", g, 0))
-                prep.append(lambda g=g: weight_pe("we", g, 1))
+                for h in range(2):
+                    prep.append(lambda g=g, h=h: weight("we", g, h, WE[g][h]))
             for h in range(2):
-                if h < WP_PE[g - 1]:
-                    prep.append(lambda g=g, h=h: weight_pe("wp", g - 1, h))
-                else:
-                    prep.append(lambda g=g, h=h: wp_vector(g - 1, h))
+                prep.append(lambda g=g, h=h: weight("wp", g - 1, h, WP[g - 1][h]))
             if g < G:
                 prep.append(lambda g=g: we_quantize(g))
             prep.append(lambda g=g: wp_quantize(g - 1))
@@ -431,56 +480,65 @@ def tile_gated_inverted_bottleneck_f3_kernel(
         def plan(step, phase, fn, *args):
             at.setdefault((step, phase), []).append((fn, args))
 
-        for s in range(TILES):
-            plan(s - 1, "T0", expand, s)
-            plan(s, "S0", ramp, s)
-            plan(s + SQ_LAG, "S1", square, s)
-        for i in range(UNITS):
-            plan(4 * i + X_LAG, "V0", shift, i)
-            plan(4 * i + X_LAG + 1, "V1", swish, i, 0)
-            plan(4 * i + X_LAG + 2, "V1", swish, i, 1)
-        last_h = -1
-        finished = {}
+        for T in range(TILES):
+            plan(T - RAMP_LEAD, "T0", expand, T)
+            plan(T - RAMP_LEAD, "S1", ramp, T)
+            plan(T - 1, "G0", clip, T)
+            plan(T, "V0", swish, T)
+            plan(T + SQ_LAG, "S0", square, T)
+        h0 = -1
+        quantized = {}
         for bt in BATCHES:
-            c0 = 4 * bt[-1] + SQ_LAG + 4
-            w = CHAIN if bt[-1] < UNITS - 1 else CHAIN_LAST
-            plan(c0 - 1, "V9", root, bt)
-            plan(c0 + w - 1, "V9", finish_root, bt)
-            h0 = max(c0 + w + 1, last_h)
+            c0 = 4 * bt[-1] + 4 + SQ_LAG
+            steps = -(-12 // CHAIN_OPS)
+            plan(c0, "V3", root_start, bt)
+            for k in range(steps):
+                plan(c0 + 1 + k, "G1", root_steps, bt, k == steps - 1)
+            c1 = c0 + 1 + steps + SG_GAP
             for i in bt:
-                plan(c0 + w, "S2", sigmoid, i)
-                plan(h0 - 1, "V8", gate_mul, i)
-                plan(h0, "V5", gated, i, 0)
-                plan(h0 + 1, "V5", gated, i, 1)
+                plan(c1, "S2", sigmoid, i)
+                plan(c1 + 1, "G2", gate_mul, i)
+                plan(c1 + 2, "T1", gate_move, i)
+            h0 = max(c1 + 2 + GATE_GAP, h0)
+            for i in bt:
+                for q in range(4):
+                    if i in SG:
+                        plan(h0 + q, "S3", gated_scalar, i, q)
+                        if q % 2:
+                            plan(h0 + q, "V1", gather, i, q // 2)
+                    else:
+                        plan(h0 + q, "V1", gated, i, q)
                 if i == LAST:
-                    plan(h0 + 1, "V6", h_quantize, i, 0, 1)
-                    plan(h0 + 2, "V6", h_quantize, i, 1, 2)
+                    plan(h0 + 2, "V2", h_quantize, i, 0, 1)
+                    plan(h0 + 4, "V2", h_quantize, i, 1, 2)
                 else:
-                    plan(h0 + 2, "V6", h_quantize, i, 0, 2)
-                plan(h0 + 4, "T1", project, i)
-                finished[i] = h0 + 4
-                h0 += H_STEP
-            last_h = h0
+                    plan(h0 + 4, "V2", h_quantize, i, 0, 2)
+                quantized[i] = h0 + 4
+                h0 += 4
         for j in range(4):
-            plan(finished[G - 1] + 1 + j // 2, "V7", finish, 0, j)
-        assert finished[G] > finished[G - 1] + 2
+            for g in range(G):
+                plan(quantized[G - 1] + 1 + 2 * j, "T2", project, g, j)
+            plan(quantized[G - 1] + 2 + 2 * j, "V4", finish, 0, j)
+        for g in range(G):
+            for j in range(4):
+                plan(max(TILES, quantized[G - 1] + 9, quantized[G + g] + 1), "T2", project, G + g, j)
         for j in range(8):
-            plan(XB_STEP + j, "V4", add_bias, j)
-        plan(0, "T2", x_transposes, 1)
+            plan(XB_STEP + j * XB_GAP, XB[j] + "5", add_bias, j)
+        plan(X1_STEP, "T3", x_transposes, 1)
         for t in range(4):
-            plan(1, "V3", affine, 1, t)
-        plan(2, "V3", u_interleave, 1)
-        plan(3, "V3", u_quantize, 1)
-        plan(5, "T2", later_parameters)
+            plan(X1_STEP, "V5", affine, 1, t)
+        plan(X1_STEP + 1, "V5", u_interleave, 1)
+        plan(X1_STEP + 2, "V5", u_quantize, 1)
+        plan(LATER_STEP, "T3", later_parameters)
 
-        for s in range(-1, finished[LAST] + 1):
-            for phase in ("T0", "T1", "T2", "S0", "S1", "S2", "V0", "V1"):
+        for s in range(-RAMP_LEAD, quantized[LAST] + 2):
+            for phase in [k for ph in PHASES for k in ((ph, "S3") if ph == "T3" else (ph,))]:
                 for fn, args in at.get((s, phase), []):
                     fn(*args)
             for event in prep[: PREP(s)]:
                 event()
                 prep.pop(0)
-            for phase in ("V3", "V4", "V5", "V6", "V7", "V8", "V9"):
+            for phase in ("V4", "V5", "G5"):
                 for fn, args in at.get((s, phase), []):
                     fn(*args)
         for j in range(4):

@@ -24,34 +24,37 @@ TILES = 4 * UNITS
 LAST = UNITS - 1
 SEED = 0x5F3759DF
 BANKS = 5
-R_BUFS = 4
+R_BUFS = 3
 A_BUFS = 6
-WP = ('VV', 'PV', 'PP', 'PV', 'PP', 'PP')
-WE = ('PP', 'VV', 'PP', 'VV', 'PV', 'PP')
+WP = ('VV', 'VV', 'VV', 'VV', 'VV', 'VV')
+WE = ('PP', 'PP', 'PP', 'PP', 'PP', 'PP')
 SQ_LAG = 2
-CHAIN_OPS = 3
-XB_STEP = 4
-XB_GAP = 2
-XB = 'VVVVVVVG'
-X1_STEP = -2
-LATER_STEP = 0
+CHAIN_OPS = 2
+XB_STEP = 24
+XB_GAP = 3
+XB = 'PPPPGGGG'
+X1_STEP = 6
+LATER_STEP = 2
 HQ_BUFS = 7
 RAMP_LEAD = 2
-SG_GAP = 1
+CHAIN_V = 0
+G_GATHER = ()
+HS_BUFS = 1
+S_AHEAD = 1
+H_PARTS = 1
+H_ODD = 0
+S_CLIP = ((1,), (2,), (1,), (2,), (1,), (2,), (1,), (2,), (1,), (0, 1, 2), (0, 1, 2), (0, 1, 2))
+SG_GAP = 0
 GATE_GAP = 0
 AFF_S = ()
-SG = (7, 10, 11)
-PHASES = ('T0', 'T1', 'T2', 'T3', 'S0', 'S1', 'S2', 'G0', 'G1', 'G2', 'V0', 'V1', 'V3', 'V2')
+SG = (10, 11)
+PHASES = ('T0', 'T1', 'T2', 'T3', 'S0', 'S1', 'S2', 'G1', 'G2', 'C0', 'V0', 'V3', 'V1', 'V2')
 BATCHES = [(0, 1), (2, 3), (4, 5), (6, 7), (8, 9), (10, 11)]
 batch_of = {i: bt for bt in BATCHES for i in bt}
 
 
 def PREP(s):
     return (3 if s < 4 else 1)
-
-
-def CLIP_V(T):
-    return False
 
 ROW_GAIN, ROW_BIAS, ROW_BE, ROWS_FIRST = 0, 1, 2, 8
 ROW_ALPHA, ROW_BETA, ROW_LAM, ROW_BP, ROWS_LATER = 0, 6, 12, 18, 18
@@ -139,6 +142,7 @@ def tile_gated_inverted_bottleneck_f3_kernel(
             return par
 
         be_c = keep.tile([P, G, 4], F32, name="be_c")
+        be_d = keep.tile([P, G, 4], F32, name="be_d")
 
         u_codes = keep.tile([P, B * S], U32, name="u_codes", align_bytes=64)
         u_scales = keep.tile([P, B * S], U8, name="u_scales", align_bytes=64)
@@ -221,6 +225,9 @@ def tile_gated_inverted_bottleneck_f3_kernel(
                      wp_raw[g][:, :, 256 * h : 256 * h + 256].rearrange("p j (c i) -> p c j i", i=4))
                 ]
             for o, src in pairs:
+                if mode == "G" and kind == "wp":
+                    o = dst.rearrange("p (c j) -> p c j", j=4)
+                    src = wp_raw[g][:, :, 256 * h : 256 * h + 256].rearrange("p j c -> p c j")
                 if mode == "V":
                     nc.vector.tensor_copy(out=o, in_=src)
                 elif mode == "S":
@@ -269,20 +276,25 @@ def tile_gated_inverted_bottleneck_f3_kernel(
             )
             e_ps[T] = bank
 
+        def on_scalar(T):
+            return T % 4 in S_CLIP[T // 4]
+
         def ramp(T):
             i, t = divmod(T, 4)
             r = work.tile([P, HALF], F32, name="r", tag="r", bufs=R_BUFS)
+            up = not on_scalar(T)
             nc.scalar.activation(
-                out=r[:], in_=e_ps[T][:], func=ACT.Relu, scale=1.0 / 6.0, bias=be_c[:, i % G, t : t + 1]
+                out=r[:], in_=e_ps[T][:], func=ACT.Relu, scale=1.0 / 6.0 if up else -1.0 / 6.0,
+                bias=(be_c if up else be_d)[:, i % G, t : t + 1],
             )
             r_sb[T] = r
 
         def clip(T):
             c = work.tile([P, HALF], F32, name="c", tag="c", bufs=R_BUFS)
-            if CLIP_V(T):
-                nc.vector.tensor_scalar(out=c[:], in0=r_sb[T][:], scalar1=1.0, scalar2=None, op0=ALU.min)
+            if on_scalar(T):
+                nc.scalar.activation(out=c[:], in_=r_sb[T][:], func=ACT.Relu, scale=-1.0, bias=one[:])
             else:
-                nc.gpsimd.tensor_scalar(out=c[:], in0=r_sb[T][:], scalar1=1.0, scalar2=1.0, op0=ALU.min, op1=ALU.mult)
+                nc.vector.tensor_scalar(out=c[:], in0=r_sb[T][:], scalar1=1.0, scalar2=None, op0=ALU.min)
             c_sb[T] = c
 
         def swish(T):
@@ -320,11 +332,13 @@ def tile_gated_inverted_bottleneck_f3_kernel(
                 out=y[0][:].bitcast(I32), in0=x[:].bitcast(I32), scalar1=-0.5, scalar2=float(SEED), op0=ALU.mult, op1=ALU.add
             )
 
+            eng = nc.vector if CHAIN_V else nc.gpsimd
+
             def mul(o, a, b):
-                return lambda: nc.gpsimd.tensor_tensor(out=o[:], in0=a[:], in1=b[:], op=ALU.mult)
+                return lambda: eng.tensor_tensor(out=o[:], in0=a[:], in1=b[:], op=ALU.mult)
 
             def affine_of(o, a, m, k):
-                return lambda: nc.gpsimd.tensor_scalar(
+                return lambda: eng.tensor_scalar(
                     out=o[:], in0=a[:], scalar1=m, scalar2=k, op0=ALU.mult, op1=ALU.add
                 )
 
@@ -343,49 +357,57 @@ def tile_gated_inverted_bottleneck_f3_kernel(
                 op()
             chains[bt] = chains[bt][count:]
 
-        def sigmoid(i):
-            g = i % G
-            bt = batch_of[i]
-            en = en_sb[bt][:, i - bt[0]]
-            sg = work.tile([P, 2, 4], F32, name="sg", tag="sg", bufs=3)
-            for t in range(4):
-                nc.scalar.activation(
-                    out=sg[:, :, t], in_=en[:, :, t], func=ACT.Sigmoid,
-                    scale=later[0][:, ROW_ALPHA + g, t : t + 1], bias=later[0][:, ROW_BETA + g, t : t + 1],
-                )
-            sg_sb[i] = sg
+        def per_batch(row, bt):
+            g = bt[0] % G
+            return later[0][:, row + g : row + g + len(bt), :].unsqueeze(2).to_broadcast([P, len(bt), 2, 4])
 
-        def gate_mul(i):
-            gate = work.tile([P, 2, 4], F32, name="gate", tag="gate", bufs=3)
-            lam_i = later[0][:, ROW_LAM + i % G, :].unsqueeze(1).to_broadcast([P, 2, 4])
-            nc.gpsimd.tensor_tensor(out=gate[:], in0=sg_sb[i][:], in1=lam_i, op=ALU.mult)
-            gate_sb[i] = gate
+        def gate_in(bt):
+            z = work.tile([P, len(bt), 2, 4], F32, name="z", tag="z", bufs=2)
+            z2 = work.tile([P, len(bt), 2, 4], F32, name="z2", tag="z2", bufs=2)
+            eng = nc.vector if CHAIN_V else nc.gpsimd
+            eng.tensor_tensor(out=z[:], in0=en_sb[bt][:], in1=per_batch(ROW_ALPHA, bt), op=ALU.mult)
+            eng.tensor_tensor(out=z2[:], in0=z[:], in1=per_batch(ROW_BETA, bt), op=ALU.add)
+            sg_sb[bt] = z2
+
+        def sigmoid(bt):
+            sg = work.tile([P, len(bt), 2, 4], F32, name="sg", tag="sg", bufs=2)
+            nc.scalar.activation(out=sg[:], in_=sg_sb[bt][:], func=ACT.Sigmoid)
+            sg_sb[bt] = sg
+
+        def gate_mul(bt):
+            gate = work.tile([P, len(bt), 2, 4], F32, name="gate", tag="gate", bufs=2)
+            eng = nc.vector if CHAIN_V else nc.gpsimd
+            eng.tensor_tensor(out=gate[:], in0=sg_sb[bt][:], in1=per_batch(ROW_LAM, bt), op=ALU.mult)
+            for i in bt:
+                gate_sb[i] = gate[:, i - bt[0]]
+            sg_sb[bt] = gate
 
         gates = gatep.tile([P, UNITS, 2, 4], F32, name="gates")
 
-        def gate_move(i):
+        def gate_move(bt):
             nc.tensor.matmul(
-                gates[:, i].rearrange("p b t -> p (b t)"), lhsT=ident_f[:],
-                rhs=gate_sb[i][:].rearrange("p b t -> p (b t)"), start=True, stop=True,
+                gates[:, bt[0] : bt[0] + len(bt)].rearrange("p u b t -> p (u b t)"), lhsT=ident_f[:],
+                rhs=sg_sb[bt][:].rearrange("p u b t -> p (u b t)"), start=True, stop=True,
             )
 
         def gated(i, q):
-            b, part = divmod(q, 2)
+            b, part = divmod(q, H_PARTS)
+            width = S // H_PARTS
             if q == 0:
                 h = work.tile([P, 2, S, 4], BF16, name="h", tag="h", align_bytes=64)
                 h_sb[i] = h
-            n0 = P * part
+            n0 = width * part
             nc.vector.tensor_tensor(
-                out=h_sb[i][:, b, n0 : n0 + P].rearrange("p (c k) t -> p c t k", k=4),
-                in0=a_sb[i][:, :, S * b + n0 : S * b + n0 + P].rearrange("p t (c k) -> p c t k", k=4),
-                in1=gates[:, i, b, :].unsqueeze(1).unsqueeze(3).to_broadcast([P, P // 4, 4, 4]),
+                out=h_sb[i][:, b, n0 : n0 + width].rearrange("p (c k) t -> p c t k", k=4),
+                in0=a_sb[i][:, :, S * b + n0 : S * b + n0 + width].rearrange("p t (c k) -> p c t k", k=4),
+                in1=gates[:, i, b, :].unsqueeze(1).unsqueeze(3).to_broadcast([P, width // 4, 4, 4]),
                 op=ALU.mult,
             )
 
         def gated_scalar(i, q):
             b, part = divmod(q, 2)
             if q == 0:
-                hs = work.tile([P, 4, HALF], BF16, name="hs", tag="hs", bufs=1)
+                hs = work.tile([P, 4, HALF], BF16, name="hs", tag="hs", bufs=HS_BUFS)
                 hs_sb[i] = hs
             for t in (2 * part, 2 * part + 1):
                 cols = slice(S * b, S * b + S)
@@ -397,6 +419,12 @@ def tile_gated_inverted_bottleneck_f3_kernel(
             if b == 0:
                 h = work.tile([P, 2, S, 4], BF16, name="h", tag="h", align_bytes=64)
                 h_sb[i] = h
+            if i in G_GATHER:
+                nc.gpsimd.tensor_scalar(
+                    out=h_sb[i][:, b], in0=hs_sb[i][:, :, S * b : S * b + S].rearrange("p t n -> p n t"),
+                    scalar1=1.0, scalar2=0.0, op0=ALU.mult, op1=ALU.add,
+                )
+                return
             nc.vector.tensor_copy(
                 out=h_sb[i][:, b].rearrange("p (c k) t -> p c t k", k=4),
                 in_=hs_sb[i][:, :, S * b : S * b + S].rearrange("p t (c k) -> p c t k", k=4),
@@ -439,13 +467,21 @@ def tile_gated_inverted_bottleneck_f3_kernel(
 
         def later_parameters():
             later[0] = transposed_rows(rows_later, ROWS_LATER, "par_later")
+            if XB == "P" * 8:
+                return
             bp_ps = accp.tile([P, C], F32, name="bp_ps", tag="acc")
             picked = ident_b[:, ROW_BP : ROW_BP + 1].to_broadcast([P, P])
             nc.tensor.matmul(bp_ps[:], lhsT=picked, rhs=rows_later[:], start=True, stop=True)
             nc.scalar.copy(out=bp_all[:], in_=bp_ps[:])
 
         def add_bias(j):
-            if XB[j] == "G":
+            if XB[j] == "P":
+                bank = accp.tile([P, C], F32, name="bank_x", tag="acc")
+                picked = ident_b[:, ROW_BP : ROW_BP + 1].to_broadcast([P, P])
+                nc.tensor.matmul(bank[:], lhsT=ident_b[:], rhs=x_sb[j // 2][:, j % 2, :], start=True, stop=False)
+                nc.tensor.matmul(bank[:], lhsT=picked, rhs=rows_later[:], start=False, stop=True)
+                nc.scalar.copy(out=xb[:, j, :], in_=bank[:])
+            elif XB[j] == "G":
                 nc.gpsimd.tensor_tensor(out=xb[:, j, :], in0=x_sb[j // 2][:, j % 2, :], in1=bp_all[:], op=ALU.add)
             else:
                 nc.vector.tensor_tensor(out=xb[:, j, :], in0=x_sb[j // 2][:, j % 2, :], in1=bp_all[:], op=ALU.add)
@@ -460,6 +496,7 @@ def tile_gated_inverted_bottleneck_f3_kernel(
             weight("we", 0, h, WE[0][h])
         be_par = par_first[:, ROW_BE : ROW_BE + G, :]
         nc.vector.tensor_scalar(out=be_c[:], in0=be_par, scalar1=1.0 / 6.0, scalar2=0.5, op0=ALU.mult, op1=ALU.add)
+        nc.vector.tensor_scalar(out=be_d[:], in0=be_par, scalar1=-1.0 / 6.0, scalar2=0.5, op0=ALU.mult, op1=ALU.add)
         u_interleave(0)
         we_quantize(0)
         u_quantize(0)
@@ -483,7 +520,7 @@ def tile_gated_inverted_bottleneck_f3_kernel(
         for T in range(TILES):
             plan(T - RAMP_LEAD, "T0", expand, T)
             plan(T - RAMP_LEAD, "S1", ramp, T)
-            plan(T - 1, "G0", clip, T)
+            plan(T - 1, "C0", clip, T)
             plan(T, "V0", swish, T)
             plan(T + SQ_LAG, "S0", square, T)
         h0 = -1
@@ -495,19 +532,22 @@ def tile_gated_inverted_bottleneck_f3_kernel(
             for k in range(steps):
                 plan(c0 + 1 + k, "G1", root_steps, bt, k == steps - 1)
             c1 = c0 + 1 + steps + SG_GAP
-            for i in bt:
-                plan(c1, "S2", sigmoid, i)
-                plan(c1 + 1, "G2", gate_mul, i)
-                plan(c1 + 2, "T1", gate_move, i)
-            h0 = max(c1 + 2 + GATE_GAP, h0)
+            plan(c1 - 1, "G2", gate_in, bt)
+            plan(c1, "S2", sigmoid, bt)
+            plan(c1 + 1, "G2", gate_mul, bt)
+            plan(c1 + 2, "T1", gate_move, bt)
+            h0 = max(c1 + 2 + GATE_GAP + S_AHEAD, h0)
             for i in bt:
                 for q in range(4):
-                    if i in SG:
-                        plan(h0 + q, "S3", gated_scalar, i, q)
+                    if i in SG or i in G_GATHER:
+                        plan(h0 + q - S_AHEAD, "S3", gated_scalar, i, q)
                         if q % 2:
-                            plan(h0 + q, "V1", gather, i, q // 2)
+                            plan(h0 + q - S_AHEAD * (i in G_GATHER), "G3" if i in G_GATHER else "V1", gather, i, q // 2)
                     else:
-                        plan(h0 + q, "V1", gated, i, q)
+                        if H_PARTS == 2:
+                            plan(h0 + q, "V1", gated, i, q)
+                        elif q % 2 == H_ODD:
+                            plan(h0 + q, "V1", gated, i, q // 2)
                 if i == LAST:
                     plan(h0 + 2, "V2", h_quantize, i, 0, 1)
                     plan(h0 + 4, "V2", h_quantize, i, 1, 2)
@@ -532,13 +572,13 @@ def tile_gated_inverted_bottleneck_f3_kernel(
         plan(LATER_STEP, "T3", later_parameters)
 
         for s in range(-RAMP_LEAD, quantized[LAST] + 2):
-            for phase in [k for ph in PHASES for k in ((ph, "S3") if ph == "T3" else (ph,))]:
+            for phase in [k for ph in PHASES for k in ((ph, "S3", "G3") if ph == "T3" else (ph,))]:
                 for fn, args in at.get((s, phase), []):
                     fn(*args)
             for event in prep[: PREP(s)]:
                 event()
                 prep.pop(0)
-            for phase in ("V4", "V5", "G5"):
+            for phase in ("V4", "V5", "G5", "P5"):
                 for fn, args in at.get((s, phase), []):
                     fn(*args)
         for j in range(4):

from contextlib import ExitStack

import concourse.mybir as mybir
from concourse.masks import make_identity

B, S, C, E = 4, 256, 512, 3072
FLOPS = 2 * 2 * B * S * C * E

F32 = mybir.dt.float32
BF16 = mybir.dt.bfloat16
U32 = mybir.dt.uint32
U8 = mybir.dt.uint8
I32 = mybir.dt.int32
E4X4 = mybir.dt.float8_e4m3fn_x4
E5X4 = mybir.dt.float8_e5m2_x4
ALU = mybir.AluOpType
ACT = mybir.ActivationFunctionType

P = 128
G = 6
HALF = 512
UNITS = 2 * G
TILES = 4 * UNITS
LAST = UNITS - 1
SEED = 0x5F3759DF
BANKS = 5
R_BUFS = 3
A_BUFS = 6
WP = ('VV', 'VV', 'VV', 'VV', 'VV', 'VV')
WE = ('PP', 'PP', 'PP', 'PP', 'PP', 'PP')
SQ_LAG = 2
CHAIN_OPS = 2
XB_STEP = 24
XB_GAP = 3
XB = 'PPPPGGGG'
X1_STEP = 6
LATER_STEP = 2
HQ_BUFS = 7
RAMP_LEAD = 2
CHAIN_V = 0
G_GATHER = ()
HS_BUFS = 1
S_AHEAD = 1
H_PARTS = 1
H_ODD = 0
S_CLIP = ((1,), (2,), (1,), (2,), (1,), (2,), (1,), (2,), (1,), (0, 1, 2), (0, 1, 2), (0, 1, 2))
SG_GAP = 0
GATE_GAP = 0
AFF_S = ()
SG = (10, 11)
PHASES = ('T0', 'T1', 'T2', 'T3', 'S0', 'S1', 'S2', 'G1', 'G2', 'C0', 'V0', 'V3', 'V1', 'V2')
BATCHES = [(0, 1), (2, 3), (4, 5), (6, 7), (8, 9), (10, 11)]
batch_of = {i: bt for bt in BATCHES for i in bt}


def PREP(s):
    return (3 if s < 4 else 1)

ROW_GAIN, ROW_BIAS, ROW_BE, ROWS_FIRST = 0, 1, 2, 8
ROW_ALPHA, ROW_BETA, ROW_LAM, ROW_BP, ROWS_LATER = 0, 6, 12, 18, 18


def tile_gated_inverted_bottleneck_f3_kernel(
    tc, x, in_gain, in_bias, we, be, alpha, beta, lam, wp, bp, out
):
    nc = tc.nc
    with ExitStack() as ctx:
        keep = ctx.enter_context(tc.tile_pool(name="keep", bufs=1))
        work = ctx.enter_context(tc.tile_pool(name="work", bufs=2))
        bankp = ctx.enter_context(tc.psum_pool(name="bankp", bufs=BANKS))
        accp = ctx.enter_context(tc.psum_pool(name="accp", bufs=7 - BANKS))
        gatep = ctx.enter_context(tc.psum_pool(name="gatep", bufs=1))
        ctx.enter_context(tc.manual_schedule())

        rows_first = keep.tile([P, C], BF16, name="rows_first")
        rows_later = keep.tile([P, C], BF16, name="rows_later")
        nc.vector.memset(rows_first[:], 0.0)
        nc.vector.memset(rows_later[:], 0.0)
        ident_f = keep.tile([P, P], F32, name="ident_f")
        ident_b = keep.tile([P, P], BF16, name="ident_b")
        one = keep.tile([P, 1], F32, name="one")
        nc.gpsimd.memset(one[:], 1.0)
        make_identity(nc, ident_f[:])
        make_identity(nc, ident_b[:])

        def load_row(queue, tile, vec, row, g0, g1):
            queue.dma_start(out=tile[row + g0 : row + g1, :], in_=vec.rearrange("(g c) -> g c", c=C)[g0:g1])

        for vec, row in ((alpha, ROW_ALPHA), (beta, ROW_BETA), (lam, ROW_LAM)):
            load_row(nc.gpsimd, rows_later, vec, row, 0, G)
        load_row(nc.gpsimd, rows_later, bp, ROW_BP, 0, 1)
        warm = keep.tile([P, 1], F32, name="warm")
        nc.scalar.activation(out=warm[:], in_=one[:], func=ACT.Sigmoid)
        x_sb = []
        we_raw = []
        wp_raw = []
        x_view = x.rearrange("(b p i) c -> b p i c", p=P, i=2)
        we_view = we.rearrange("(p j) e -> p j e", j=4)
        wp_view = wp.rearrange("(g p j) c -> g p j c", p=P, j=4)

        def load_x(b):
            t = keep.tile([P, 2, C], BF16, name="x%d" % b)
            nc.sync.dma_start(out=t[:], in_=x_view[b])
            x_sb.append(t)

        def load_we(g):
            t = work.tile([P, 4, 512], BF16, name="we_raw_t", tag="we_raw", bufs=4)
            nc.sync.dma_start(out=t[:], in_=we_view[:, :, 512 * g : 512 * g + 512])
            we_raw.append(t)

        def load_wp(g):
            t = work.tile([P, 4, C], BF16, name="wp_raw_t", tag="wp_raw", bufs=4)
            nc.sync.dma_start(out=t[:], in_=wp_view[g])
            wp_raw.append(t)

        load_row(nc.sync, rows_first, in_gain, ROW_GAIN, 0, 1)
        load_row(nc.sync, rows_first, in_bias, ROW_BIAS, 0, 1)
        load_x(0)
        load_x(1)
        load_row(nc.sync, rows_first, be, ROW_BE, 0, 4)
        load_row(nc.sync, rows_first, be, ROW_BE, 4, G)
        load_we(0)
        load_x(2)
        load_x(3)
        load_we(1)
        load_wp(0)
        for g in range(2, G):
            load_we(g)
            load_wp(g - 1)
        load_wp(G - 1)

        def transposed_rows(rows, count, label):
            words = rows[:].bitcast(F32)
            pt = accp.tile([P, 2 * P], F32, name="pt", tag="acc")
            for u in range(2):
                nc.tensor.transpose(pt[:, P * u : P * u + P], words[:, u::2], ident_f[:])
            par = keep.tile([P, count, 4], F32, name=label)
            nc.vector.tensor_copy(
                out=par[:].rearrange("p r (u e) -> p r u e", e=2),
                in_=pt[:].bitcast(BF16).rearrange("p (u r e) -> p r u e", u=2, e=2)[:, :count],
            )
            return par

        be_c = keep.tile([P, G, 4], F32, name="be_c")
        be_d = keep.tile([P, G, 4], F32, name="be_d")

        u_codes = keep.tile([P, B * S], U32, name="u_codes", align_bytes=64)
        u_scales = keep.tile([P, B * S], U8, name="u_scales", align_bytes=64)
        we_codes = keep.tile([P, E], U32, name="we_codes", align_bytes=64)
        we_scales = keep.tile([P, E], U8, name="we_scales", align_bytes=64)
        wp_codes = keep.tile([P, G, C], U32, name="wp_codes", align_bytes=64)
        wp_scales = keep.tile([P, G, C], U8, name="wp_scales", align_bytes=64)
        xb = keep.tile([P, 2 * B, C], F32, name="xb")
        bp_all = keep.tile([P, C], F32, name="bp_all")

        xt = {}
        ut = {}

        def x_transposes(n):
            for u in range(2):
                t = (bankp if n == 0 else accp).tile([P, HALF], F32, name="xt", tag="bank" if n == 0 else "acc")
                for j in range(4):
                    words = x_sb[2 * n + j // 2][:].rearrange("p i c -> p (i c)").bitcast(F32)
                    w0 = (C // 2) * (j % 2)
                    nc.tensor.transpose(t[:, P * j : P * j + P], words[:, w0 + u : w0 + C // 2 : 2], ident_f[:])
                xt[n, u] = t

        def affine(n, t):
            if n not in ut:
                u_tile = work.tile([P, 4, HALF], BF16, name="ut", tag="ut")
                ut[n] = u_tile
            u, e = divmod(t, 2)
            src = xt[n, u][:].bitcast(BF16).rearrange("p (c e) -> p e c", e=2)[:, e, :]
            dst = ut[n][:, t, :]
            gain = par_first[:, ROW_GAIN, t : t + 1]
            bias = par_first[:, ROW_BIAS, t : t + 1]
            if u == 1 or n in AFF_S:
                nc.scalar.activation(out=dst, in_=src, func=ACT.Identity, scale=gain, bias=bias)
            else:
                nc.vector.tensor_scalar(out=dst, in0=src, scalar1=gain, scalar2=bias, op0=ALU.mult, op1=ALU.add)

        ui = {}

        def u_interleave(n):
            t = work.tile([P, 4 * HALF], BF16, name="ui", tag="ui", align_bytes=64)
            nc.vector.tensor_copy(
                out=t[:].rearrange("p (c i t) -> p c t i", i=4, t=4),
                in_=ut[n][:].rearrange("p t (c i) -> p c t i", i=4),
            )
            ui[n] = t

        def u_quantize(n):
            cols = slice(HALF * n, HALF * n + HALF)
            nc.vector.quantize_mx(out=u_codes[:, cols].bitcast(E4X4), scales=u_scales[:, cols], in_=ui[n][:])

        wi = {}

        def wi_half(kind, g, h):
            if (kind, g) not in wi:
                t = work.tile([P, 2048], BF16, name="wi_" + kind, tag="wi_" + kind, align_bytes=64)
                wi[kind, g] = t
            return wi[kind, g][:, 1024 * h : 1024 * h + 1024]

        def weight_pe(kind, g, h):
            bank = bankp.tile([P, 1024], BF16, name="bank_w", tag="bank")
            for q in (2 * h, 2 * h + 1):
                if kind == "we":
                    view = we_raw[g][:].rearrange("p j (m t) -> p t m j", t=4)[:, q]
                else:
                    view = wp_raw[g][:, :, P * q : P * q + P].rearrange("p j c -> p c j")
                o = 512 * (q % 2)
                nc.tensor.matmul(bank[:, o : o + 512], lhsT=ident_b[:], rhs=view, start=True, stop=True)
            nc.scalar.copy(out=wi_half(kind, g, h), in_=bank[:])

        def weight_sb(kind, g, h, mode):
            dst = wi_half(kind, g, h)
            if kind == "we":
                pairs = [
                    (dst[:, 512 * k : 512 * k + 512].rearrange("p (m j) -> p m j", j=4),
                     we_raw[g][:].rearrange("p j (m t) -> p t m j", t=4)[:, 2 * h + k]) for k in range(2)
                ]
            else:
                pairs = [
                    (dst.rearrange("p (c i j) -> p c j i", i=4, j=4),
                     wp_raw[g][:, :, 256 * h : 256 * h + 256].rearrange("p j (c i) -> p c j i", i=4))
                ]
            for o, src in pairs:
                if mode == "G" and kind == "wp":
                    o = dst.rearrange("p (c j) -> p c j", j=4)
                    src = wp_raw[g][:, :, 256 * h : 256 * h + 256].rearrange("p j c -> p c j")
                if mode == "V":
                    nc.vector.tensor_copy(out=o, in_=src)
                elif mode == "S":
                    nc.scalar.copy(out=o, in_=src)
                else:
                    nc.gpsimd.tensor_scalar(out=o, in0=src, scalar1=1.0, scalar2=0.0, op0=ALU.mult, op1=ALU.add)

        def weight(kind, g, h, mode):
            if mode == "P":
                weight_pe(kind, g, h)
            else:
                weight_sb(kind, g, h, mode)

        def we_quantize(g):
            cols = slice(512 * g, 512 * g + 512)
            nc.vector.quantize_mx(out=we_codes[:, cols].bitcast(E4X4), scales=we_scales[:, cols], in_=wi["we", g][:])

        def wp_quantize(g):
            nc.vector.quantize_mx(out=wp_codes[:, g, :].bitcast(E4X4), scales=wp_scales[:, g, :], in_=wi["wp", g][:])

        e_ps = {}
        r_sb = {}
        c_sb = {}
        a_sb = {}
        ms_sb = {}
        en_sb = {}
        chains = {}
        sg_sb = {}
        gate_sb = {}
        gate_ps = {}
        h_sb = {}
        hs_sb = {}
        hq = {}
        acc = {}
        later = {}

        def expand(T):
            i, t = divmod(T, 4)
            n, g = divmod(i, G)
            bank = bankp.tile([P, HALF], F32, name="bank_e", tag="bank")
            m = slice(512 * g + P * t, 512 * g + P * t + P)
            k = slice(HALF * n, HALF * n + HALF)
            nc.tensor.matmul_mx(
                out=bank[:], lhsT=we_codes[:, m].bitcast(E4X4), lhsT_scale=we_scales[:, m],
                rhs=u_codes[:, k].bitcast(E4X4), rhs_scale=u_scales[:, k], start=True, stop=True,
            )
            e_ps[T] = bank

        def on_scalar(T):
            return T % 4 in S_CLIP[T // 4]

        def ramp(T):
            i, t = divmod(T, 4)
            r = work.tile([P, HALF], F32, name="r", tag="r", bufs=R_BUFS)
            up = not on_scalar(T)
            nc.scalar.activation(
                out=r[:], in_=e_ps[T][:], func=ACT.Relu, scale=1.0 / 6.0 if up else -1.0 / 6.0,
                bias=(be_c if up else be_d)[:, i % G, t : t + 1],
            )
            r_sb[T] = r

        def clip(T):
            c = work.tile([P, HALF], F32, name="c", tag="c", bufs=R_BUFS)
            if on_scalar(T):
                nc.scalar.activation(out=c[:], in_=r_sb[T][:], func=ACT.Relu, scale=-1.0, bias=one[:])
            else:
                nc.vector.tensor_scalar(out=c[:], in0=r_sb[T][:], scalar1=1.0, scalar2=None, op0=ALU.min)
            c_sb[T] = c

        def swish(T):
            i, t = divmod(T, 4)
            if t == 0:
                a = work.tile([P, 4, HALF], F32, name="a", tag="a", bufs=A_BUFS)
                a_sb[i] = a
            nc.vector.scalar_tensor_tensor(
                out=a_sb[i][:, t, :], in0=e_ps[T][:], scalar=par_first[:, ROW_BE + i % G, t : t + 1], in1=c_sb[T][:],
                op0=ALU.add, op1=ALU.mult,
            )

        def square(T):
            i, t = divmod(T, 4)
            bt = batch_of[i]
            if t == 0 and i == bt[0]:
                ms = work.tile([P, len(bt), 2, 4], F32, name="ms", tag="ms", bufs=3)
                ms_sb[bt] = ms
            for b in range(2):
                junk = work.tile([P, S], F32, name="junk", tag="junk")
                nc.scalar.activation(
                    out=junk[:], in_=a_sb[i][:, t, S * b : S * b + S], func=ACT.Square, scale=1.0 / 16.0,
                    accum_out=ms_sb[bt][:, i - bt[0], b, t : t + 1],
                )

        def root_start(bt):
            x = ms_sb[bt]
            shape = [P, len(bt), 2, 4]
            y = [work.tile(shape, F32, name="y%d" % k, tag="y%d" % k, bufs=2) for k in range(2)]
            w = work.tile(shape, F32, name="w", tag="w", bufs=2)
            v = work.tile(shape, F32, name="v", tag="v", bufs=2)
            q = work.tile(shape, F32, name="q", tag="q", bufs=2)
            en = work.tile(shape, F32, name="en", tag="en", bufs=2)
            nc.vector.tensor_scalar(
                out=y[0][:].bitcast(I32), in0=x[:].bitcast(I32), scalar1=-0.5, scalar2=float(SEED), op0=ALU.mult, op1=ALU.add
            )

            eng = nc.vector if CHAIN_V else nc.gpsimd

            def mul(o, a, b):
                return lambda: eng.tensor_tensor(out=o[:], in0=a[:], in1=b[:], op=ALU.mult)

            def affine_of(o, a, m, k):
                return lambda: eng.tensor_scalar(
                    out=o[:], in0=a[:], scalar1=m, scalar2=k, op0=ALU.mult, op1=ALU.add
                )

            ops = []
            for k in range(2):
                ops += [
                    mul(w, x, y[k]), mul(v, w, y[k]), affine_of(q, v, 0.375, -1.25), mul(v, q, v),
                    affine_of(q, v, 1.0, 1.875), mul((y[1], en)[k], q, (y[0], w)[k]),
                ]
            chains[bt] = ops
            en_sb[bt] = en

        def root_steps(bt, last):
            count = len(chains[bt]) if last else CHAIN_OPS
            for op in chains[bt][:count]:
                op()
            chains[bt] = chains[bt][count:]

        def per_batch(row, bt):
            g = bt[0] % G
            return later[0][:, row + g : row + g + len(bt), :].unsqueeze(2).to_broadcast([P, len(bt), 2, 4])

        def gate_in(bt):
            z = work.tile([P, len(bt), 2, 4], F32, name="z", tag="z", bufs=2)
            z2 = work.tile([P, len(bt), 2, 4], F32, name="z2", tag="z2", bufs=2)
            eng = nc.vector if CHAIN_V else nc.gpsimd
            eng.tensor_tensor(out=z[:], in0=en_sb[bt][:], in1=per_batch(ROW_ALPHA, bt), op=ALU.mult)
            eng.tensor_tensor(out=z2[:], in0=z[:], in1=per_batch(ROW_BETA, bt), op=ALU.add)
            sg_sb[bt] = z2

        def sigmoid(bt):
            sg = work.tile([P, len(bt), 2, 4], F32, name="sg", tag="sg", bufs=2)
            nc.scalar.activation(out=sg[:], in_=sg_sb[bt][:], func=ACT.Sigmoid)
            sg_sb[bt] = sg

        def gate_mul(bt):
            gate = work.tile([P, len(bt), 2, 4], F32, name="gate", tag="gate", bufs=2)
            eng = nc.vector if CHAIN_V else nc.gpsimd
            eng.tensor_tensor(out=gate[:], in0=sg_sb[bt][:], in1=per_batch(ROW_LAM, bt), op=ALU.mult)
            for i in bt:
                gate_sb[i] = gate[:, i - bt[0]]
            sg_sb[bt] = gate

        gates = gatep.tile([P, UNITS, 2, 4], F32, name="gates")

        def gate_move(bt):
            nc.tensor.matmul(
                gates[:, bt[0] : bt[0] + len(bt)].rearrange("p u b t -> p (u b t)"), lhsT=ident_f[:],
                rhs=sg_sb[bt][:].rearrange("p u b t -> p (u b t)"), start=True, stop=True,
            )

        def gated(i, q):
            b, part = divmod(q, H_PARTS)
            width = S // H_PARTS
            if q == 0:
                h = work.tile([P, 2, S, 4], BF16, name="h", tag="h", align_bytes=64)
                h_sb[i] = h
            n0 = width * part
            nc.vector.tensor_tensor(
                out=h_sb[i][:, b, n0 : n0 + width].rearrange("p (c k) t -> p c t k", k=4),
                in0=a_sb[i][:, :, S * b + n0 : S * b + n0 + width].rearrange("p t (c k) -> p c t k", k=4),
                in1=gates[:, i, b, :].unsqueeze(1).unsqueeze(3).to_broadcast([P, width // 4, 4, 4]),
                op=ALU.mult,
            )

        def gated_scalar(i, q):
            b, part = divmod(q, 2)
            if q == 0:
                hs = work.tile([P, 4, HALF], BF16, name="hs", tag="hs", bufs=HS_BUFS)
                hs_sb[i] = hs
            for t in (2 * part, 2 * part + 1):
                cols = slice(S * b, S * b + S)
                nc.scalar.activation(
                    out=hs_sb[i][:, t, cols], in_=a_sb[i][:, t, cols], func=ACT.Copy, scale=gate_sb[i][:, b, t : t + 1]
                )

        def gather(i, b):
            if b == 0:
                h = work.tile([P, 2, S, 4], BF16, name="h", tag="h", align_bytes=64)
                h_sb[i] = h
            if i in G_GATHER:
                nc.gpsimd.tensor_scalar(
                    out=h_sb[i][:, b], in0=hs_sb[i][:, :, S * b : S * b + S].rearrange("p t n -> p n t"),
                    scalar1=1.0, scalar2=0.0, op0=ALU.mult, op1=ALU.add,
                )
                return
            nc.vector.tensor_copy(
                out=h_sb[i][:, b].rearrange("p (c k) t -> p c t k", k=4),
                in_=hs_sb[i][:, :, S * b : S * b + S].rearrange("p t (c k) -> p c t k", k=4),
            )

        def h_quantize(i, b0, b1):
            if b0 == 0:
                codes = work.tile([P, HALF], U32, name="h_codes", tag="h_codes", align_bytes=64, bufs=HQ_BUFS)
                scales = work.tile([P, HALF], U8, name="h_scales", tag="h_scales", align_bytes=64, bufs=HQ_BUFS)
                hq[i] = (codes, scales)
            codes, scales = hq[i]
            cols = slice(S * b0, S * b1)
            nc.vector.quantize_mx(
                out=codes[:, cols].bitcast(E5X4), scales=scales[:, cols],
                in_=h_sb[i][:].rearrange("p b n t -> p (b n t)")[:, 4 * S * b0 : 4 * S * b1],
            )

        def project(i, j):
            n, g = divmod(i, G)
            codes, scales = hq[i]
            if g == 0:
                if j < 7 - BANKS or n == 0:
                    t = accp.tile([P, C], F32, name="acc", tag="acc")
                else:
                    t = bankp.tile([P, C], F32, name="acc_b", tag="bank")
                acc[n, j] = t
            m = slice(P * j, P * j + P)
            nc.tensor.matmul_mx(
                out=acc[n, j][:], lhsT=codes[:, m].bitcast(E5X4), lhsT_scale=scales[:, m],
                rhs=wp_codes[:, g, :].bitcast(E4X4), rhs_scale=wp_scales[:, g, :],
                start=(g == 0), stop=(g == G - 1),
            )

        out_view = out.rearrange("(b p i) c -> b i p c", p=P, i=2)

        def finish(n, j):
            o = work.tile([P, C], F32, name="o", tag="o", bufs=4)
            nc.vector.tensor_tensor(out=o[:], in0=acc[n, j][:], in1=xb[:, 4 * n + j, :], op=ALU.add)
            nc.sync.dma_start(out=out_view[2 * n + j // 2, j % 2], in_=o[:])

        def later_parameters():
            later[0] = transposed_rows(rows_later, ROWS_LATER, "par_later")
            if XB == "P" * 8:
                return
            bp_ps = accp.tile([P, C], F32, name="bp_ps", tag="acc")
            picked = ident_b[:, ROW_BP : ROW_BP + 1].to_broadcast([P, P])
            nc.tensor.matmul(bp_ps[:], lhsT=picked, rhs=rows_later[:], start=True, stop=True)
            nc.scalar.copy(out=bp_all[:], in_=bp_ps[:])

        def add_bias(j):
            if XB[j] == "P":
                bank = accp.tile([P, C], F32, name="bank_x", tag="acc")
                picked = ident_b[:, ROW_BP : ROW_BP + 1].to_broadcast([P, P])
                nc.tensor.matmul(bank[:], lhsT=ident_b[:], rhs=x_sb[j // 2][:, j % 2, :], start=True, stop=False)
                nc.tensor.matmul(bank[:], lhsT=picked, rhs=rows_later[:], start=False, stop=True)
                nc.scalar.copy(out=xb[:, j, :], in_=bank[:])
            elif XB[j] == "G":
                nc.gpsimd.tensor_tensor(out=xb[:, j, :], in0=x_sb[j // 2][:, j % 2, :], in1=bp_all[:], op=ALU.add)
            else:
                nc.vector.tensor_tensor(out=xb[:, j, :], in0=x_sb[j // 2][:, j % 2, :], in1=bp_all[:], op=ALU.add)

        x_transposes(0)
        par_first = transposed_rows(rows_first, ROWS_FIRST, "par_first")
        affine(0, 2)
        affine(0, 0)
        affine(0, 3)
        affine(0, 1)
        for h in range(2):
            weight("we", 0, h, WE[0][h])
        be_par = par_first[:, ROW_BE : ROW_BE + G, :]
        nc.vector.tensor_scalar(out=be_c[:], in0=be_par, scalar1=1.0 / 6.0, scalar2=0.5, op0=ALU.mult, op1=ALU.add)
        nc.vector.tensor_scalar(out=be_d[:], in0=be_par, scalar1=-1.0 / 6.0, scalar2=0.5, op0=ALU.mult, op1=ALU.add)
        u_interleave(0)
        we_quantize(0)
        u_quantize(0)

        prep = []
        for g in range(1, G + 1):
            if g < G:
                for h in range(2):
                    prep.append(lambda g=g, h=h: weight("we", g, h, WE[g][h]))
            for h in range(2):
                prep.append(lambda g=g, h=h: weight("wp", g - 1, h, WP[g - 1][h]))
            if g < G:
                prep.append(lambda g=g: we_quantize(g))
            prep.append(lambda g=g: wp_quantize(g - 1))

        at = {}

        def plan(step, phase, fn, *args):
            at.setdefault((step, phase), []).append((fn, args))

        for T in range(TILES):
            plan(T - RAMP_LEAD, "T0", expand, T)
            plan(T - RAMP_LEAD, "S1", ramp, T)
            plan(T - 1, "C0", clip, T)
            plan(T, "V0", swish, T)
            plan(T + SQ_LAG, "S0", square, T)
        h0 = -1
        quantized = {}
        for bt in BATCHES:
            c0 = 4 * bt[-1] + 4 + SQ_LAG
            steps = -(-12 // CHAIN_OPS)
            plan(c0, "V3", root_start, bt)
            for k in range(steps):
                plan(c0 + 1 + k, "G1", root_steps, bt, k == steps - 1)
            c1 = c0 + 1 + steps + SG_GAP
            plan(c1 - 1, "G2", gate_in, bt)
            plan(c1, "S2", sigmoid, bt)
            plan(c1 + 1, "G2", gate_mul, bt)
            plan(c1 + 2, "T1", gate_move, bt)
            h0 = max(c1 + 2 + GATE_GAP + S_AHEAD, h0)
            for i in bt:
                for q in range(4):
                    if i in SG or i in G_GATHER:
                        plan(h0 + q - S_AHEAD, "S3", gated_scalar, i, q)
                        if q % 2:
                            plan(h0 + q - S_AHEAD * (i in G_GATHER), "G3" if i in G_GATHER else "V1", gather, i, q // 2)
                    else:
                        if H_PARTS == 2:
                            plan(h0 + q, "V1", gated, i, q)
                        elif q % 2 == H_ODD:
                            plan(h0 + q, "V1", gated, i, q // 2)
                if i == LAST:
                    plan(h0 + 2, "V2", h_quantize, i, 0, 1)
                    plan(h0 + 4, "V2", h_quantize, i, 1, 2)
                else:
                    plan(h0 + 4, "V2", h_quantize, i, 0, 2)
                quantized[i] = h0 + 4
                h0 += 4
        for j in range(4):
            for g in range(G):
                plan(quantized[G - 1] + 1 + 2 * j, "T2", project, g, j)
            plan(quantized[G - 1] + 2 + 2 * j, "V4", finish, 0, j)
        for g in range(G):
            for j in range(4):
                plan(max(TILES, quantized[G - 1] + 9, quantized[G + g] + 1), "T2", project, G + g, j)
        for j in range(8):
            plan(XB_STEP + j * XB_GAP, XB[j] + "5", add_bias, j)
        plan(X1_STEP, "T3", x_transposes, 1)
        for t in range(4):
            plan(X1_STEP, "V5", affine, 1, t)
        plan(X1_STEP + 1, "V5", u_interleave, 1)
        plan(X1_STEP + 2, "V5", u_quantize, 1)
        plan(LATER_STEP, "T3", later_parameters)

        for s in range(-RAMP_LEAD, quantized[LAST] + 2):
            for phase in [k for ph in PHASES for k in ((ph, "S3", "G3") if ph == "T3" else (ph,))]:
                for fn, args in at.get((s, phase), []):
                    fn(*args)
            for event in prep[: PREP(s)]:
                event()
                prep.pop(0)
            for phase in ("V4", "V5", "G5", "P5"):
                for fn, args in at.get((s, phase), []):
                    fn(*args)
        for j in range(4):
            finish(1, j)
